import numpy as np
import ml_dtypes


def mxq(x, axis, fmt="e4m3"):
    dtype, down = {"e4m3": (ml_dtypes.float8_e4m3fn, 7), "e5m2": (ml_dtypes.float8_e5m2, 14)}[fmt]
    v = np.moveaxis(np.asarray(x, np.float32).astype(ml_dtypes.bfloat16).astype(np.float64), axis, -1)
    blocks = v.reshape(v.shape[:-1] + (-1, 32))
    amax = np.abs(blocks).max(-1, keepdims=True)
    byte = np.maximum(np.where(amax > 0, np.frexp(amax)[1] - 1 + 127, 0) - down, 1)
    scale = np.exp2(byte - 127.0)
    codes = (blocks / scale).astype(np.float32).astype(dtype).astype(np.float64)
    return np.moveaxis((codes * scale).reshape(v.shape), -1, axis)


WIDE = False


def mx_kscale(k):
    if not WIDE:
        return np.ones(k)
    levels = np.array([10, -10, 5, -5, 0])
    if k % 512:
        return np.exp2(np.random.permutation(np.resize(levels, k // 32))).repeat(32)
    a = np.empty((k // 512, 16))
    for p in range(k // 512):
        a[p, :8] = np.random.permutation(np.resize(levels, 8))
        for g in range(8):
            far = levels[np.abs(levels - a[p, g]) >= 10]
            a[p, g + 8] = far[np.random.randint(len(far))]
    return np.exp2(a.ravel()).repeat(32)


def f64(x):
    return np.asarray(x).astype(np.float64)


def striped8(idx):
    return np.concatenate([x.reshape(-1, 16).T for x in idx]).astype(np.uint16)


def runs(offs, k):
    lists = np.stack([offs[16 * r : 16 * r + 16].T.reshape(-1) for r in range(8)]).astype(np.int64)
    return lists[np.arange(k) % 512 // 64]


def pack_weight(w):
    k, n = w.shape
    w = f64(np.asarray(w, np.float32).astype(ml_dtypes.bfloat16)).reshape(k // 32, 32, n)
    amax = np.abs(w).max(1)
    byte = np.clip(np.where(amax > 0, np.frexp(amax)[1] - 1 + 127 - 7, 1), 1, 254)
    scaled = (w * np.exp2(127.0 - byte)[:, None, :]).reshape(k, n).astype(np.float32)
    words = np.ascontiguousarray(scaled.reshape(k // 512, 128, 4, n).transpose(0, 1, 3, 2)).astype(ml_dtypes.float8_e4m3fn).view(np.uint8)
    return words, np.ascontiguousarray(byte.astype(np.uint8).reshape(k // 512, 16, n))


def unpack_weight(words, scales):
    g, p, n, _ = words.shape
    vals = np.ascontiguousarray(words).view(ml_dtypes.float8_e4m3fn).astype(np.float64) * np.repeat(np.exp2(scales.astype(np.float64) - 127.0), 8, axis=1)[..., None]
    return vals.transpose(0, 1, 3, 2).reshape(g * 512, n)


E2M1 = np.array([0.0, 0.5, 1.0, 1.5, 2.0, 3.0, 4.0, 6.0, -0.0, -0.5, -1.0, -1.5, -2.0, -3.0, -4.0, -6.0])


def pack_fp4(w):
    k, n = w.shape
    w = f64(np.asarray(w, np.float32).astype(ml_dtypes.bfloat16)).reshape(k // 32, 32, n)
    amax = np.abs(w).max(1)
    mant, ex = np.frexp(amax / 6.0)
    byte = np.clip(np.where(amax > 0, np.where(mant > 0.5, ex, ex - 1) + 127, 1), 1, 254)
    scaled = (w * np.exp2(127.0 - byte)[:, None, :]).reshape(k, n).astype(np.float32)
    c = np.ascontiguousarray(scaled.reshape(k // 512, 128, 4, n).transpose(0, 1, 3, 2)).astype(ml_dtypes.float4_e2m1fn).view(np.uint8) & 0xF
    words = (c[..., 0::2] | (c[..., 1::2] << 4)).reshape(k // 512, 128, 2 * n)
    return np.ascontiguousarray(words), np.ascontiguousarray(byte.astype(np.uint8).reshape(k // 512, 16, n))


def unpack_fp4(words, scales):
    g, _, n = scales.shape
    words = np.ascontiguousarray(words).reshape(g, 128, n, 2)
    nib = np.empty((g, 128, n, 4), np.uint8)
    nib[..., 0::2] = words & 0xF
    nib[..., 1::2] = words >> 4
    vals = E2M1[nib] * np.repeat(np.exp2(scales.astype(np.float64) - 127.0), 8, axis=1)[..., None]
    return vals.transpose(0, 1, 3, 2).reshape(g * 512, n)


def gelu(v):
    return 0.5 * v * (1.0 + np.tanh(np.sqrt(2.0 / np.pi) * (v + 0.044715 * v**3)))


K, T, S, H, N = 1024, 2048, 512, 512, 128


def setup_inputs():
    n = np.random.standard_normal
    s = mx_kscale(K)[:, None]
    u = mx_kscale(H)
    packed_xT = pack_weight(n((K, T)) * s)
    packed_w2 = pack_fp4(n((H, N)) / np.sqrt(H) / u[:, None])
    return {
        "x_words": packed_xT[0],
        "x_scales": packed_xT[1],
        "w1": (n((K, H)) / np.sqrt(K) / s * u).astype(np.float32),
        "w2_words": packed_w2[0],
        "w2_scales": packed_w2[1],
        "offs": striped8(np.stack([np.random.permutation(T)[:S] for _ in range(8)])),
    }


def reference(x_words, x_scales, w1, w2_words, w2_scales, offs):
    xq = unpack_weight(x_words, x_scales)[np.arange(K)[:, None], runs(offs, K)]
    h = gelu(mxq(f64(w1), 0, "e4m3").T @ xq)
    return unpack_fp4(w2_words, w2_scales).T @ mxq(h, 0, "e4m3")

@@ -1,0 +1,121 @@
+from contextlib import ExitStack
+
+import concourse.mybir as mybir
+
+K, T, S, H, N = 1024, 2048, 512, 512, 128
+FLOPS = 2 * K * H * S + 2 * H * N * S
+
+F32 = mybir.dt.float32
+BF16 = mybir.dt.bfloat16
+I32 = mybir.dt.int32
+U32 = mybir.dt.uint32
+U16 = mybir.dt.uint16
+U8 = mybir.dt.uint8
+FP8X4 = mybir.dt.float8_e4m3fn_x4
+FP4X4 = mybir.dt.float4_e2m1fn_x4
+GELU = mybir.ActivationFunctionType.Gelu_apprx_tanh
+
+P = 128
+PACK = 4
+PASSES = K // (P * PACK)
+HALF = 256
+CHUNK = 128
+CHUNKS = S // CHUNK
+M_SPLIT = 64
+
+
+def tile_picked_phmlp_gelu_p_kernel(tc, x_words, x_scales, w1, w2_words, w2_scales, offs, out):
+    nc = tc.nc
+    with ExitStack() as ctx:
+        keep = ctx.enter_context(tc.tile_pool(name="keep", bufs=1))
+        psum = ctx.enter_context(tc.psum_pool(name="psum", bufs=1))
+
+        lists = keep.tile([P, S // 16], U16, name="lists")
+        nc.sync.dma_start(lists[:], offs)
+        w2_codes = keep.tile([P, 2 * N], U8, name="w2_codes", align_bytes=64)
+        nc.sync.dma_start(w2_codes[:].bitcast(I32), w2_words[0].bitcast(I32))
+
+        w1_rows = [w1[512 * z : 512 * (z + 1), :].rearrange("(p j) c -> p j c", j=PACK) for z in range(PASSES)]
+        w1_raw = [keep.tile([P, PACK, H], F32, name="w1_raw0")]
+        nc.scalar.dma_start(w1_raw[0][:], w1_rows[0])
+
+        scale_table = keep.tile([P, T], U8, name="scale_table")
+        nc.vector.memset(scale_table[:].bitcast(I32), 0)
+        nc.sync.dma_start(scale_table[0:P:4, :].bitcast(I32), x_scales.bitcast(I32).rearrange("z q c -> q z c"))
+
+        warm_in = keep.tile([P, 1], F32, name="warm_in", tag="w1_raw1")
+        warm_bias = keep.tile([P, 1], F32, name="warm_bias", tag="x_table1")
+        warm_out = keep.tile([P, 1], F32, name="warm_out", tag="x_table0")
+        nc.vector.memset(warm_in[:], 0.0)
+        nc.vector.memset(warm_bias[:], 0.0)
+        nc.scalar.activation(warm_out[:], warm_in[:], GELU, bias=warm_bias[:])
+
+        w1_raw.append(keep.tile([P, PACK, H], F32, name="w1_raw1", tag="w1_raw1"))
+        nc.scalar.dma_start(w1_raw[1][:], w1_rows[1])
+        x_table = [keep.tile([P, T], I32, name=f"x_table{z}", tag=f"x_table{z}") for z in range(PASSES)]
+        for z in range(PASSES):
+            nc.scalar.dma_start(x_table[z][:], x_words[z].rearrange("p n t -> p (n t)").bitcast(I32))
+
+        picked_scales = keep.tile([P, S], U8, name="picked_scales", tag="picked_scales", align_bytes=64)
+        nc.vector.tensor_copy(picked_scales[:], scale_table[:].indirect(lists[:]))
+        x_planes = keep.tile([P, S], U8, name="x_planes", align_bytes=64)
+        nc.vector.tensor_copy(x_planes[:].bitcast(I32), picked_scales[:].bitcast(I32))
+        for i in range(1, 4):
+            nc.sync.dma_start(x_planes[i : i + 101 : 4, :].bitcast(I32), picked_scales[8 * i : 8 * i + 101 : 4, :].bitcast(I32))
+
+        w2_plane = keep.tile([P, N], U8, name="w2_plane", tag="picked_scales", align_bytes=64)
+        nc.gpsimd.memset(w2_plane[:].bitcast(I32), 0)
+        for q in range(4):
+            nc.sync.dma_start(w2_plane[32 * q : 32 * q + 4, :].bitcast(I32), w2_scales[0, 4 * q : 4 * q + 4, :].bitcast(I32))
+
+        w1_codes, w1_planes = [], []
+        for z in range(PASSES):
+            grouped = keep.tile([P, PACK, P, PACK], BF16, name=f"w1_grouped{z}", align_bytes=64)
+            dst = grouped[:].rearrange("p t m j -> p m t j")
+            src = w1_raw[z][:].rearrange("p j (m t) -> p m t j", t=PACK)
+            nc.scalar.copy(dst[:, :M_SPLIT], src[:, :M_SPLIT])
+            nc.vector.tensor_copy(dst[:, M_SPLIT:], src[:, M_SPLIT:])
+            codes = keep.tile([P, H], U32, name=f"w1_codes{z}", align_bytes=64)
+            plane = keep.tile([P, H], U8, name=f"w1_plane{z}", align_bytes=64)
+            nc.vector.quantize_mx(out=codes[:].bitcast(FP8X4), scales=plane[:], in_=grouped[:].rearrange("p t m j -> p (t m j)"))
+            w1_codes.append(codes)
+            w1_planes.append(plane)
+
+        hidden = [psum.tile([P, PACK, CHUNK], F32, name=f"hidden{c}") for c in range(CHUNKS)]
+        for z in range(PASSES):
+            for half in range(S // HALF):
+                picked = keep.tile([P, HALF], U32, name=f"picked{z}{half}", align_bytes=64)
+                cols = slice(half * HALF // 16, (half + 1) * HALF // 16)
+                nc.vector.tensor_copy(picked[:], x_table[z][:].bitcast(U32).indirect(lists[:, cols]))
+                for part in range(HALF // CHUNK):
+                    c = half * (HALF // CHUNK) + part
+                    for t in range(PACK):
+                        nc.tensor.matmul_mx(
+                            out=hidden[c][:, t, :],
+                            lhsT=w1_codes[z][:, t * P : (t + 1) * P].bitcast(FP8X4),
+                            lhsT_scale=w1_planes[z][:, t * P : (t + 1) * P],
+                            rhs=picked[:, part * CHUNK : (part + 1) * CHUNK].bitcast(FP8X4),
+                            rhs_scale=x_planes[4 * z : P, c * CHUNK : (c + 1) * CHUNK],
+                            start=(z == 0 and t == 0),
+                            stop=(z == PASSES - 1 and t == PACK - 1),
+                        )
+
+        for c in range(CHUNKS):
+            h_grouped = keep.tile([P, CHUNK, PACK], BF16, name=f"h_grouped{c}", align_bytes=64)
+            nc.scalar.activation(h_grouped[:], hidden[c][:].rearrange("p t n -> p n t"), GELU)
+            h_codes = keep.tile([P, CHUNK], U32, name=f"h_codes{c}", align_bytes=64)
+            h_plane = keep.tile([P, CHUNK], U8, name=f"h_plane{c}", align_bytes=64)
+            nc.vector.quantize_mx(out=h_codes[:].bitcast(FP8X4), scales=h_plane[:], in_=h_grouped[:].rearrange("p n t -> p (n t)"))
+            acc = psum.tile([N, CHUNK], F32, name=f"acc{c}")
+            nc.tensor.matmul_mx(
+                out=acc[:],
+                lhsT=w2_codes[:].bitcast(FP4X4),
+                lhsT_scale=w2_plane[:],
+                rhs=h_codes[:].bitcast(FP8X4),
+                rhs_scale=h_plane[:],
+                start=True,
+                stop=True,
+            )
+            result = keep.tile([N, CHUNK], F32, name=f"result{c}")
+            nc.vector.tensor_copy(result[:], acc[:])
+            nc.sync.dma_start(out[:, c * CHUNK : (c + 1) * CHUNK], result[:])

@@ -39,34 +39,36 @@ def tile_picked_phmlp_gelu_p_kernel(tc, x_words, x_scales, w1, w2_words, w2_scal
         w1_raw = [keep.tile([P, PACK, H], F32, name="w1_raw0")]
         nc.scalar.dma_start(w1_raw[0][:], w1_rows[0])
 
-        scale_table = keep.tile([P, T], U8, name="scale_table")
+        scale_table = keep.tile([P, T], U8, name="scale_table", tag="scale_table", align_bytes=64)
         nc.vector.memset(scale_table[:].bitcast(I32), 0)
         nc.sync.dma_start(scale_table[0:P:4, :].bitcast(I32), x_scales.bitcast(I32).rearrange("z q c -> q z c"))
 
         warm_in = keep.tile([P, 1], F32, name="warm_in", tag="w1_raw1")
-        warm_bias = keep.tile([P, 1], F32, name="warm_bias", tag="x_table1")
         warm_out = keep.tile([P, 1], F32, name="warm_out", tag="x_table0")
         nc.vector.memset(warm_in[:], 0.0)
-        nc.vector.memset(warm_bias[:], 0.0)
-        nc.scalar.activation(warm_out[:], warm_in[:], GELU, bias=warm_bias[:])
+        nc.scalar.activation(warm_out[:], warm_in[:], GELU)
 
         w1_raw.append(keep.tile([P, PACK, H], F32, name="w1_raw1", tag="w1_raw1"))
         nc.scalar.dma_start(w1_raw[1][:], w1_rows[1])
-        x_table = [keep.tile([P, T], I32, name=f"x_table{z}", tag=f"x_table{z}") for z in range(PASSES)]
-        for z in range(PASSES):
-            nc.scalar.dma_start(x_table[z][:], x_words[z].rearrange("p n t -> p (n t)").bitcast(I32))
+        x_rows = [x_words[z].rearrange("p n t -> p (n t)").bitcast(I32) for z in range(PASSES)]
+        x_table = [keep.tile([P, T], I32, name="x_table0", tag="x_table0")]
+        nc.scalar.dma_start(x_table[0][:], x_rows[0])
 
-        picked_scales = keep.tile([P, S], U8, name="picked_scales", tag="picked_scales", align_bytes=64)
+        picked_scales = keep.tile([P, S], U8, name="picked_scales", tag="x_table1", align_bytes=64)
         nc.vector.tensor_copy(picked_scales[:], scale_table[:].indirect(lists[:]))
         x_planes = keep.tile([P, S], U8, name="x_planes", align_bytes=64)
         nc.vector.tensor_copy(x_planes[:].bitcast(I32), picked_scales[:].bitcast(I32))
-        for i in range(1, 4):
-            nc.sync.dma_start(x_planes[i : i + 101 : 4, :].bitcast(I32), picked_scales[8 * i : 8 * i + 101 : 4, :].bitcast(I32))
+        for z in range(PASSES):
+            for i in range(1, 4):
+                nc.sync.dma_start(x_planes[4 * z + i : P : 32, :].bitcast(I32), x_planes[4 * z + 8 * i : P : 32, :].bitcast(I32))
+        x_table.append(keep.tile([P, T], I32, name="x_table1", tag="x_table1", align_bytes=64))
+        nc.sync.dma_start(x_table[1][:], x_rows[1])
 
-        w2_plane = keep.tile([P, N], U8, name="w2_plane", tag="picked_scales", align_bytes=64)
-        nc.gpsimd.memset(w2_plane[:].bitcast(I32), 0)
+        w2_plane = keep.tile([P, N], U8, name="w2_plane", tag="scale_table", align_bytes=64)
+        nc.vector.memset(w2_plane[:].bitcast(I32), 0)
         for q in range(4):
             nc.sync.dma_start(w2_plane[32 * q : 32 * q + 4, :].bitcast(I32), w2_scales[0, 4 * q : 4 * q + 4, :].bitcast(I32))
+
 
         w1_codes, w1_planes = [], []
         for z in range(PASSES):

@@ -32,24 +32,25 @@ def tile_picked_phmlp_gelu_p_kernel(tc, x_words, x_scales, w1, w2_words, w2_scal
 
         lists = keep.tile([P, S // 16], U16, name="lists")
         nc.sync.dma_start(lists[:], offs)
-        w2_codes = keep.tile([P, 2 * N], U8, name="w2_codes", align_bytes=64)
-        nc.sync.dma_start(w2_codes[:].bitcast(I32), w2_words[0].bitcast(I32))
 
         w1_rows = [w1[512 * z : 512 * (z + 1), :].rearrange("(p j) c -> p j c", j=PACK) for z in range(PASSES)]
-        w1_raw = [keep.tile([P, PACK, H], F32, name="w1_raw0")]
-        nc.scalar.dma_start(w1_raw[0][:], w1_rows[0])
+        w1_raw = [keep.tile([P, PACK, H], F32, name="w1_raw0", tag="w1_raw0", align_bytes=64)]
+        for j in range(0, PACK, 2):
+            nc.scalar.dma_start(w1_raw[0][:, j : j + 2], w1_rows[0][:, j : j + 2])
 
         scale_table = keep.tile([P, T], U8, name="scale_table", tag="scale_table", align_bytes=64)
         nc.vector.memset(scale_table[:].bitcast(I32), 0)
         nc.sync.dma_start(scale_table[0:P:4, :].bitcast(I32), x_scales.bitcast(I32).rearrange("z q c -> q z c"))
 
-        warm_in = keep.tile([P, 1], F32, name="warm_in", tag="w1_raw1")
-        warm_out = keep.tile([P, 1], F32, name="warm_out", tag="x_table0")
-        nc.vector.memset(warm_in[:], 0.0)
-        nc.scalar.activation(warm_out[:], warm_in[:], GELU)
-
+        warm_seed = keep.tile([P, 1], F32, name="warm_seed", tag="w1_raw1")
+        warm_in = keep.tile([P, 1], F32, name="warm_in", tag="x_table0")
+        warm_out = keep.tile([P, 1], F32, name="warm_out")
+        nc.vector.memset(warm_seed[:], 0.0)
+        nc.vector.tensor_copy(warm_in[:], warm_seed[:])
         w1_raw.append(keep.tile([P, PACK, H], F32, name="w1_raw1", tag="w1_raw1"))
         nc.scalar.dma_start(w1_raw[1][:], w1_rows[1])
+        nc.scalar.activation(warm_out[:], warm_in[:], GELU)
+
         x_rows = [x_words[z].rearrange("p n t -> p (n t)").bitcast(I32) for z in range(PASSES)]
         x_table = [keep.tile([P, T], I32, name="x_table0", tag="x_table0")]
         nc.scalar.dma_start(x_table[0][:], x_rows[0])
@@ -82,6 +83,9 @@ def tile_picked_phmlp_gelu_p_kernel(tc, x_words, x_scales, w1, w2_words, w2_scal
             nc.vector.quantize_mx(out=codes[:].bitcast(FP8X4), scales=plane[:], in_=grouped[:].rearrange("p t m j -> p (t m j)"))
             w1_codes.append(codes)
             w1_planes.append(plane)
+
+        w2_codes = keep.tile([P, 2 * N], U8, name="w2_codes", tag="w1_raw0", align_bytes=64)
+        nc.sync.dma_start(w2_codes[:].bitcast(I32), w2_words[0].bitcast(I32))
 
         hidden = [psum.tile([P, PACK, CHUNK], F32, name=f"hidden{c}") for c in range(CHUNKS)]
         for z in range(PASSES):

@@ -30,46 +30,39 @@ def tile_picked_phmlp_gelu_p_kernel(tc, x_words, x_scales, w1, w2_words, w2_scal
         keep = ctx.enter_context(tc.tile_pool(name="keep", bufs=1))
         psum = ctx.enter_context(tc.psum_pool(name="psum", bufs=1))
 
-        lists = keep.tile([P, S // 16], U16, name="lists")
-        nc.sync.dma_start(lists[:], offs)
-
         w1_rows = [w1[512 * z : 512 * (z + 1), :].rearrange("(p j) c -> p j c", j=PACK) for z in range(PASSES)]
-        w1_raw = [keep.tile([P, PACK, H], F32, name="w1_raw0", tag="w1_raw0", align_bytes=64)]
-        for j in range(0, PACK, 2):
-            nc.scalar.dma_start(w1_raw[0][:, j : j + 2], w1_rows[0][:, j : j + 2])
+        x_rows = [x_words[z].rearrange("p n t -> p (n t)").bitcast(I32) for z in range(PASSES)]
 
         scale_table = keep.tile([P, T], U8, name="scale_table", tag="scale_table", align_bytes=64)
         nc.vector.memset(scale_table[:].bitcast(I32), 0)
-        nc.sync.dma_start(scale_table[0:P:4, :].bitcast(I32), x_scales.bitcast(I32).rearrange("z q c -> q z c"))
 
-        warm_seed = keep.tile([P, 1], F32, name="warm_seed", tag="w1_raw1")
-        warm_in = keep.tile([P, 1], F32, name="warm_in", tag="x_table0")
+        w1_raw = [keep.tile([P, PACK, H], F32, name=f"w1_raw{z}", tag=f"w1_raw{z}", align_bytes=64) for z in range(PASSES)]
+        nc.sync.dma_start(w1_raw[0][:, 0:1], w1_rows[0][:, 0:1])
+        lists = keep.tile([P, S // 16], U16, name="lists")
+        nc.sync.dma_start(lists[:], offs)
+        nc.sync.dma_start(w1_raw[0][:, 1:2], w1_rows[0][:, 1:2])
+        nc.sync.dma_start(scale_table[0:P:4, :].bitcast(I32), x_scales.bitcast(I32).rearrange("z q c -> q z c"))
+        nc.sync.dma_start(w1_raw[0][:, 2:4], w1_rows[0][:, 2:4])
+        nc.sync.dma_start(w1_raw[1][:], w1_rows[1])
+        x_table = [keep.tile([P, T], I32, name="x_table0")]
+        nc.sync.dma_start(x_table[0][:], x_rows[0])
+
+        warm_in = keep.tile([P, 1], F32, name="warm_in")
         warm_out = keep.tile([P, 1], F32, name="warm_out")
-        nc.vector.memset(warm_seed[:], 0.0)
-        nc.vector.tensor_copy(warm_in[:], warm_seed[:])
-        w1_raw.append(keep.tile([P, PACK, H], F32, name="w1_raw1", tag="w1_raw1"))
-        nc.scalar.dma_start(w1_raw[1][:], w1_rows[1])
+        nc.vector.memset(warm_in[:], 0.0)
         nc.scalar.activation(warm_out[:], warm_in[:], GELU)
 
-        x_rows = [x_words[z].rearrange("p n t -> p (n t)").bitcast(I32) for z in range(PASSES)]
-        x_table = [keep.tile([P, T], I32, name="x_table0", tag="x_table0")]
-        nc.scalar.dma_start(x_table[0][:], x_rows[0])
-
-        picked_scales = keep.tile([P, S], U8, name="picked_scales", tag="x_table1", align_bytes=64)
+        x_planes = keep.tile([P, PASSES, S], U8, name="x_planes", align_bytes=64)
+        nc.vector.memset(x_planes[:].rearrange("p z s -> p (z s)").bitcast(I32), 0)
+        picked_scales = keep.tile([P, S], U8, name="picked_scales", align_bytes=64)
         nc.vector.tensor_copy(picked_scales[:], scale_table[:].indirect(lists[:]))
-        x_planes = keep.tile([P, S], U8, name="x_planes", align_bytes=64)
-        nc.vector.tensor_copy(x_planes[:].bitcast(I32), picked_scales[:].bitcast(I32))
-        for z in range(PASSES):
-            for i in range(1, 4):
-                nc.sync.dma_start(x_planes[4 * z + i : P : 32, :].bitcast(I32), x_planes[4 * z + 8 * i : P : 32, :].bitcast(I32))
-        x_table.append(keep.tile([P, T], I32, name="x_table1", tag="x_table1", align_bytes=64))
-        nc.sync.dma_start(x_table[1][:], x_rows[1])
-
-        w2_plane = keep.tile([P, N], U8, name="w2_plane", tag="scale_table", align_bytes=64)
-        nc.vector.memset(w2_plane[:].bitcast(I32), 0)
         for q in range(4):
-            nc.sync.dma_start(w2_plane[32 * q : 32 * q + 4, :].bitcast(I32), w2_scales[0, 4 * q : 4 * q + 4, :].bitcast(I32))
-
+            nc.sync.dma_start(
+                x_planes[32 * q : 32 * q + 4].rearrange("p z s -> p (z s)").bitcast(I32),
+                picked_scales[32 * q : 32 * q + 32 : 4, :].bitcast(I32),
+            )
+        x_table.append(keep.tile([P, T], I32, name="x_table1", tag="scale_table", align_bytes=64))
+        nc.sync.dma_start(x_table[1][:], x_rows[1])
 
         w1_codes, w1_planes = [], []
         for z in range(PASSES):
@@ -86,6 +79,10 @@ def tile_picked_phmlp_gelu_p_kernel(tc, x_words, x_scales, w1, w2_words, w2_scal
 
         w2_codes = keep.tile([P, 2 * N], U8, name="w2_codes", tag="w1_raw0", align_bytes=64)
         nc.sync.dma_start(w2_codes[:].bitcast(I32), w2_words[0].bitcast(I32))
+        w2_plane = keep.tile([P, N], U8, name="w2_plane", tag="w1_raw1", align_bytes=64)
+        nc.vector.memset(w2_plane[:].bitcast(I32), 0)
+        for q in range(4):
+            nc.sync.dma_start(w2_plane[32 * q : 32 * q + 4, :].bitcast(I32), w2_scales[0, 4 * q : 4 * q + 4, :].bitcast(I32))
 
         hidden = [psum.tile([P, PACK, CHUNK], F32, name=f"hidden{c}") for c in range(CHUNKS)]
         for z in range(PASSES):
@@ -101,7 +98,7 @@ def tile_picked_phmlp_gelu_p_kernel(tc, x_words, x_scales, w1, w2_words, w2_scal
                             lhsT=w1_codes[z][:, t * P : (t + 1) * P].bitcast(FP8X4),
                             lhsT_scale=w1_planes[z][:, t * P : (t + 1) * P],
                             rhs=picked[:, part * CHUNK : (part + 1) * CHUNK].bitcast(FP8X4),
-                            rhs_scale=x_planes[4 * z : P, c * CHUNK : (c + 1) * CHUNK],
+                            rhs_scale=x_planes[:, z, c * CHUNK : (c + 1) * CHUNK],
                             start=(z == 0 and t == 0),
                             stop=(z == PASSES - 1 and t == PACK - 1),
                         )

@@ -21,31 +21,30 @@ PASSES = K // (P * PACK)
 HALF = 256
 CHUNK = 128
 CHUNKS = S // CHUNK
-M_SPLIT = 64
 
 
 def tile_picked_phmlp_gelu_p_kernel(tc, x_words, x_scales, w1, w2_words, w2_scales, offs, out):
     nc = tc.nc
     with ExitStack() as ctx:
         keep = ctx.enter_context(tc.tile_pool(name="keep", bufs=1))
+        shared = ctx.enter_context(tc.tile_pool(name="shared", bufs=1))
         psum = ctx.enter_context(tc.psum_pool(name="psum", bufs=1))
 
         w1_rows = [w1[512 * z : 512 * (z + 1), :].rearrange("(p j) c -> p j c", j=PACK) for z in range(PASSES)]
         x_rows = [x_words[z].rearrange("p n t -> p (n t)").bitcast(I32) for z in range(PASSES)]
 
-        scale_table = keep.tile([P, T], U8, name="scale_table", tag="scale_table", align_bytes=64)
+        scale_table = shared.tile([P, T], U8, name="scale_table", align_bytes=64, offset=1024)
         nc.vector.memset(scale_table[:].bitcast(I32), 0)
 
-        w1_raw = [keep.tile([P, PACK, H], F32, name=f"w1_raw{z}", tag=f"w1_raw{z}", align_bytes=64) for z in range(PASSES)]
-        nc.sync.dma_start(w1_raw[0][:, 0:1], w1_rows[0][:, 0:1])
+        x_table = [keep.tile([P, T], I32, name="x_table0")]
+        nc.sync.dma_start(x_table[0][:, : T // 2], x_rows[0][:, : T // 2])
         lists = keep.tile([P, S // 16], U16, name="lists")
         nc.sync.dma_start(lists[:], offs)
-        nc.sync.dma_start(w1_raw[0][:, 1:2], w1_rows[0][:, 1:2])
+        nc.sync.dma_start(x_table[0][:, T // 2 :], x_rows[0][:, T // 2 :])
         nc.sync.dma_start(scale_table[0:P:4, :].bitcast(I32), x_scales.bitcast(I32).rearrange("z q c -> q z c"))
-        nc.sync.dma_start(w1_raw[0][:, 2:4], w1_rows[0][:, 2:4])
-        nc.sync.dma_start(w1_raw[1][:], w1_rows[1])
-        x_table = [keep.tile([P, T], I32, name="x_table0")]
-        nc.sync.dma_start(x_table[0][:], x_rows[0])
+        w1_raw = [keep.tile([P, PACK, H], F32, name=f"w1_raw{z}", tag=f"w1_raw{z}", align_bytes=64) for z in range(PASSES)]
+        for z in range(PASSES):
+            nc.sync.dma_start(w1_raw[z][:], w1_rows[z])
 
         warm_in = keep.tile([P, 1], F32, name="warm_in")
         warm_out = keep.tile([P, 1], F32, name="warm_out")
@@ -61,21 +60,22 @@ def tile_picked_phmlp_gelu_p_kernel(tc, x_words, x_scales, w1, w2_words, w2_scal
                 x_planes[32 * q : 32 * q + 4].rearrange("p z s -> p (z s)").bitcast(I32),
                 picked_scales[32 * q : 32 * q + 32 : 4, :].bitcast(I32),
             )
-        x_table.append(keep.tile([P, T], I32, name="x_table1", tag="scale_table", align_bytes=64))
+        x_table.append(shared.tile([P, T], I32, name="x_table1", align_bytes=64, offset=2112))
         nc.sync.dma_start(x_table[1][:], x_rows[1])
 
-        w1_codes, w1_planes = [], []
+        w1_codes, w1_planes = {}, {}
         for z in range(PASSES):
-            grouped = keep.tile([P, PACK, P, PACK], BF16, name=f"w1_grouped{z}", align_bytes=64)
-            dst = grouped[:].rearrange("p t m j -> p m t j")
-            src = w1_raw[z][:].rearrange("p j (m t) -> p m t j", t=PACK)
-            nc.scalar.copy(dst[:, :M_SPLIT], src[:, :M_SPLIT])
-            nc.vector.tensor_copy(dst[:, M_SPLIT:], src[:, M_SPLIT:])
-            codes = keep.tile([P, H], U32, name=f"w1_codes{z}", align_bytes=64)
-            plane = keep.tile([P, H], U8, name=f"w1_plane{z}", align_bytes=64)
-            nc.vector.quantize_mx(out=codes[:].bitcast(FP8X4), scales=plane[:], in_=grouped[:].rearrange("p t m j -> p (t m j)"))
-            w1_codes.append(codes)
-            w1_planes.append(plane)
+            src = w1_raw[z][:].rearrange("p j (m t) -> p m j t", t=PACK)
+            for pair in range(PACK // 2):
+                grouped = keep.tile([P, 2, P, PACK], BF16, name=f"w1_grouped{z}{pair}", align_bytes=64)
+                cast = nc.vector.tensor_copy if pair == 0 else nc.scalar.copy
+                cast(grouped[:].rearrange("p t m j -> p m j t"), src[:, :, :, 2 * pair : 2 * pair + 2])
+                codes = keep.tile([P, 2 * P], U32, name=f"w1_codes{z}{pair}", align_bytes=64)
+                plane = keep.tile([P, 2 * P], U8, name=f"w1_plane{z}{pair}", align_bytes=64)
+                nc.vector.quantize_mx(out=codes[:].bitcast(FP8X4), scales=plane[:], in_=grouped[:].rearrange("p t m j -> p (t m j)"))
+                for e in range(2):
+                    w1_codes[z, 2 * pair + e] = codes[:, e * P : (e + 1) * P]
+                    w1_planes[z, 2 * pair + e] = plane[:, e * P : (e + 1) * P]
 
         w2_codes = keep.tile([P, 2 * N], U8, name="w2_codes", tag="w1_raw0", align_bytes=64)
         nc.sync.dma_start(w2_codes[:].bitcast(I32), w2_words[0].bitcast(I32))
@@ -87,7 +87,10 @@ def tile_picked_phmlp_gelu_p_kernel(tc, x_words, x_scales, w1, w2_words, w2_scal
         hidden = [psum.tile([P, PACK, CHUNK], F32, name=f"hidden{c}") for c in range(CHUNKS)]
         for z in range(PASSES):
             for half in range(S // HALF):
-                picked = keep.tile([P, HALF], U32, name=f"picked{z}{half}", align_bytes=64)
+                if z == 0:
+                    picked = shared.tile([P, HALF], U32, name=f"picked{z}{half}", align_bytes=64, offset=64 if half == 0 else 1088)
+                else:
+                    picked = keep.tile([P, HALF], U32, name=f"picked{z}{half}", align_bytes=64)
                 cols = slice(half * HALF // 16, (half + 1) * HALF // 16)
                 nc.vector.tensor_copy(picked[:], x_table[z][:].bitcast(U32).indirect(lists[:, cols]))
                 for part in range(HALF // CHUNK):
@@ -95,8 +98,8 @@ def tile_picked_phmlp_gelu_p_kernel(tc, x_words, x_scales, w1, w2_words, w2_scal
                     for t in range(PACK):
                         nc.tensor.matmul_mx(
                             out=hidden[c][:, t, :],
-                            lhsT=w1_codes[z][:, t * P : (t + 1) * P].bitcast(FP8X4),
-                            lhsT_scale=w1_planes[z][:, t * P : (t + 1) * P],
+                            lhsT=w1_codes[z, t].bitcast(FP8X4),
+                            lhsT_scale=w1_planes[z, t],
                             rhs=picked[:, part * CHUNK : (part + 1) * CHUNK].bitcast(FP8X4),
                             rhs_scale=x_planes[:, z, c * CHUNK : (c + 1) * CHUNK],
                             start=(z == 0 and t == 0),
@@ -106,7 +109,7 @@ def tile_picked_phmlp_gelu_p_kernel(tc, x_words, x_scales, w1, w2_words, w2_scal
         for c in range(CHUNKS):
             h_grouped = keep.tile([P, CHUNK, PACK], BF16, name=f"h_grouped{c}", align_bytes=64)
             nc.scalar.activation(h_grouped[:], hidden[c][:].rearrange("p t n -> p n t"), GELU)
-            h_codes = keep.tile([P, CHUNK], U32, name=f"h_codes{c}", align_bytes=64)
+            h_codes = keep.tile([P, CHUNK], U32, name=f"h_codes{c}", tag="h_codes", bufs=2, align_bytes=64)
             h_plane = keep.tile([P, CHUNK], U8, name=f"h_plane{c}", align_bytes=64)
             nc.vector.quantize_mx(out=h_codes[:].bitcast(FP8X4), scales=h_plane[:], in_=h_grouped[:].rearrange("p n t -> p (n t)"))
             acc = psum.tile([N, CHUNK], F32, name=f"acc{c}")

@@ -51,19 +51,22 @@ def tile_picked_phmlp_gelu_p_kernel(tc, x_words, x_scales, w1, w2_words, w2_scal
         nc.vector.memset(warm_in[:], 0.0)
         nc.scalar.activation(warm_out[:], warm_in[:], GELU)
 
-        x_planes = keep.tile([P, PASSES, S], U8, name="x_planes", align_bytes=64)
-        nc.vector.memset(x_planes[:].rearrange("p z s -> p (z s)").bitcast(I32), 0)
+        x_planes = [keep.tile([P, S], U8, name=f"x_plane{z}", align_bytes=64) for z in range(PASSES)]
+        for z in range(PASSES):
+            nc.vector.memset(x_planes[z][:].bitcast(I32), 0)
         picked_scales = keep.tile([P, S], U8, name="picked_scales", align_bytes=64)
         nc.vector.tensor_copy(picked_scales[:], scale_table[:].indirect(lists[:]))
-        for q in range(4):
-            nc.sync.dma_start(
-                x_planes[32 * q : 32 * q + 4].rearrange("p z s -> p (z s)").bitcast(I32),
-                picked_scales[32 * q : 32 * q + 32 : 4, :].bitcast(I32),
-            )
         x_table.append(shared.tile([P, T], I32, name="x_table1", align_bytes=64, offset=2112))
-        nc.sync.dma_start(x_table[1][:], x_rows[1])
+        for z in range(PASSES):
+            for q in range(4):
+                nc.sync.dma_start(
+                    x_planes[z][32 * q : 32 * q + 4, :].bitcast(I32),
+                    picked_scales[32 * q + 4 * z : 32 * q + 32 : 8, :].bitcast(I32),
+                )
+            if z == 0:
+                nc.sync.dma_start(x_table[1][:], x_rows[1])
 
-        w1_codes, w1_planes = {}, {}
+        w1_codes, w1_planes, w1_pairs = {}, {}, {}
         for z in range(PASSES):
             src = w1_raw[z][:].rearrange("p j (m t) -> p m j t", t=PACK)
             for pair in range(PACK // 2):
@@ -73,6 +76,7 @@ def tile_picked_phmlp_gelu_p_kernel(tc, x_words, x_scales, w1, w2_words, w2_scal
                 codes = keep.tile([P, 2 * P], U32, name=f"w1_codes{z}{pair}", align_bytes=64)
                 plane = keep.tile([P, 2 * P], U8, name=f"w1_plane{z}{pair}", align_bytes=64)
                 nc.vector.quantize_mx(out=codes[:].bitcast(FP8X4), scales=plane[:], in_=grouped[:].rearrange("p t m j -> p (t m j)"))
+                w1_pairs[z, pair] = (codes[:], plane[:])
                 for e in range(2):
                     w1_codes[z, 2 * pair + e] = codes[:, e * P : (e + 1) * P]
                     w1_planes[z, 2 * pair + e] = plane[:, e * P : (e + 1) * P]
@@ -83,6 +87,18 @@ def tile_picked_phmlp_gelu_p_kernel(tc, x_words, x_scales, w1, w2_words, w2_scal
         nc.vector.memset(w2_plane[:].bitcast(I32), 0)
         for q in range(4):
             nc.sync.dma_start(w2_plane[32 * q : 32 * q + 4, :].bitcast(I32), w2_scales[0, 4 * q : 4 * q + 4, :].bitcast(I32))
+
+        warm_acc = psum.tile([P, 2 * P], F32, name="warm_acc", tag="acc3")
+        for e in range(3):
+            nc.tensor.matmul_mx(
+                out=warm_acc[:],
+                lhsT=w1_codes[0, e].bitcast(FP8X4),
+                lhsT_scale=w1_planes[0, e],
+                rhs=w1_pairs[0, e // 2][0].bitcast(FP8X4),
+                rhs_scale=w1_pairs[0, e // 2][1],
+                start=True,
+                stop=True,
+            )
 
         hidden = [psum.tile([P, PACK, CHUNK], F32, name=f"hidden{c}") for c in range(CHUNKS)]
         for z in range(PASSES):
@@ -101,7 +117,7 @@ def tile_picked_phmlp_gelu_p_kernel(tc, x_words, x_scales, w1, w2_words, w2_scal
                             lhsT=w1_codes[z, t].bitcast(FP8X4),
                             lhsT_scale=w1_planes[z, t],
                             rhs=picked[:, part * CHUNK : (part + 1) * CHUNK].bitcast(FP8X4),
-                            rhs_scale=x_planes[:, z, c * CHUNK : (c + 1) * CHUNK],
+                            rhs_scale=x_planes[z][:, c * CHUNK : (c + 1) * CHUNK],
                             start=(z == 0 and t == 0),
                             stop=(z == PASSES - 1 and t == PACK - 1),
                         )
@@ -112,7 +128,7 @@ def tile_picked_phmlp_gelu_p_kernel(tc, x_words, x_scales, w1, w2_words, w2_scal
             h_codes = keep.tile([P, CHUNK], U32, name=f"h_codes{c}", tag="h_codes", bufs=2, align_bytes=64)
             h_plane = keep.tile([P, CHUNK], U8, name=f"h_plane{c}", align_bytes=64)
             nc.vector.quantize_mx(out=h_codes[:].bitcast(FP8X4), scales=h_plane[:], in_=h_grouped[:].rearrange("p n t -> p (n t)"))
-            acc = psum.tile([N, CHUNK], F32, name=f"acc{c}")
+            acc = psum.tile([N, CHUNK], F32, name=f"acc{c}", tag=f"acc{c}")
             nc.tensor.matmul_mx(
                 out=acc[:],
                 lhsT=w2_codes[:].bitcast(FP4X4),

@@ -18,9 +18,14 @@ GELU = mybir.ActivationFunctionType.Gelu_apprx_tanh
 P = 128
 PACK = 4
 PASSES = K // (P * PACK)
+QUADRANTS = 4
 HALF = 256
 CHUNK = 128
 CHUNKS = S // CHUNK
+
+SCALE_TABLE_AT = 1024
+PICKED_AT = (64, 64 + 4 * HALF)
+LAST_TABLE_AT = 64 + 2 * 4 * HALF
 
 
 def tile_picked_phmlp_gelu_p_kernel(tc, x_words, x_scales, w1, w2_words, w2_scales, offs, out):
@@ -33,14 +38,13 @@ def tile_picked_phmlp_gelu_p_kernel(tc, x_words, x_scales, w1, w2_words, w2_scal
         w1_rows = [w1[512 * z : 512 * (z + 1), :].rearrange("(p j) c -> p j c", j=PACK) for z in range(PASSES)]
         x_rows = [x_words[z].rearrange("p n t -> p (n t)").bitcast(I32) for z in range(PASSES)]
 
-        scale_table = shared.tile([P, T], U8, name="scale_table", align_bytes=64, offset=1024)
+        scale_table = shared.tile([P, T], U8, name="scale_table", align_bytes=64, offset=SCALE_TABLE_AT)
         nc.vector.memset(scale_table[:].bitcast(I32), 0)
 
         x_table = [keep.tile([P, T], I32, name="x_table0")]
-        nc.sync.dma_start(x_table[0][:, : T // 2], x_rows[0][:, : T // 2])
+        nc.sync.dma_start(x_table[0][:], x_rows[0])
         lists = keep.tile([P, S // 16], U16, name="lists")
         nc.sync.dma_start(lists[:], offs)
-        nc.sync.dma_start(x_table[0][:, T // 2 :], x_rows[0][:, T // 2 :])
         nc.sync.dma_start(scale_table[0:P:4, :].bitcast(I32), x_scales.bitcast(I32).rearrange("z q c -> q z c"))
         w1_raw = [keep.tile([P, PACK, H], F32, name=f"w1_raw{z}", tag=f"w1_raw{z}", align_bytes=64) for z in range(PASSES)]
         for z in range(PASSES):
@@ -56,17 +60,17 @@ def tile_picked_phmlp_gelu_p_kernel(tc, x_words, x_scales, w1, w2_words, w2_scal
             nc.vector.memset(x_planes[z][:].bitcast(I32), 0)
         picked_scales = keep.tile([P, S], U8, name="picked_scales", align_bytes=64)
         nc.vector.tensor_copy(picked_scales[:], scale_table[:].indirect(lists[:]))
-        x_table.append(shared.tile([P, T], I32, name="x_table1", align_bytes=64, offset=2112))
+        x_table.append(shared.tile([P, T], I32, name="x_table1", align_bytes=64, offset=LAST_TABLE_AT))
         for z in range(PASSES):
-            for q in range(4):
+            if z == PASSES - 1:
+                nc.sync.dma_start(x_table[z][:], x_rows[z])
+            for q in range(QUADRANTS):
                 nc.sync.dma_start(
                     x_planes[z][32 * q : 32 * q + 4, :].bitcast(I32),
                     picked_scales[32 * q + 4 * z : 32 * q + 32 : 8, :].bitcast(I32),
                 )
-            if z == 0:
-                nc.sync.dma_start(x_table[1][:], x_rows[1])
 
-        w1_codes, w1_planes, w1_pairs = {}, {}, {}
+        w1_codes, w1_planes = {}, {}
         for z in range(PASSES):
             src = w1_raw[z][:].rearrange("p j (m t) -> p m j t", t=PACK)
             for pair in range(PACK // 2):
@@ -76,7 +80,6 @@ def tile_picked_phmlp_gelu_p_kernel(tc, x_words, x_scales, w1, w2_words, w2_scal
                 codes = keep.tile([P, 2 * P], U32, name=f"w1_codes{z}{pair}", align_bytes=64)
                 plane = keep.tile([P, 2 * P], U8, name=f"w1_plane{z}{pair}", align_bytes=64)
                 nc.vector.quantize_mx(out=codes[:].bitcast(FP8X4), scales=plane[:], in_=grouped[:].rearrange("p t m j -> p (t m j)"))
-                w1_pairs[z, pair] = (codes[:], plane[:])
                 for e in range(2):
                     w1_codes[z, 2 * pair + e] = codes[:, e * P : (e + 1) * P]
                     w1_planes[z, 2 * pair + e] = plane[:, e * P : (e + 1) * P]
@@ -85,30 +88,18 @@ def tile_picked_phmlp_gelu_p_kernel(tc, x_words, x_scales, w1, w2_words, w2_scal
         nc.sync.dma_start(w2_codes[:].bitcast(I32), w2_words[0].bitcast(I32))
         w2_plane = keep.tile([P, N], U8, name="w2_plane", tag="w1_raw1", align_bytes=64)
         nc.vector.memset(w2_plane[:].bitcast(I32), 0)
-        for q in range(4):
+        for q in range(QUADRANTS):
             nc.sync.dma_start(w2_plane[32 * q : 32 * q + 4, :].bitcast(I32), w2_scales[0, 4 * q : 4 * q + 4, :].bitcast(I32))
-
-        warm_acc = psum.tile([P, 2 * P], F32, name="warm_acc", tag="acc3")
-        for e in range(3):
-            nc.tensor.matmul_mx(
-                out=warm_acc[:],
-                lhsT=w1_codes[0, e].bitcast(FP8X4),
-                lhsT_scale=w1_planes[0, e],
-                rhs=w1_pairs[0, e // 2][0].bitcast(FP8X4),
-                rhs_scale=w1_pairs[0, e // 2][1],
-                start=True,
-                stop=True,
-            )
 
         hidden = [psum.tile([P, PACK, CHUNK], F32, name=f"hidden{c}") for c in range(CHUNKS)]
         for z in range(PASSES):
             for half in range(S // HALF):
                 if z == 0:
-                    picked = shared.tile([P, HALF], U32, name=f"picked{z}{half}", align_bytes=64, offset=64 if half == 0 else 1088)
+                    picked = shared.tile([P, HALF], U32, name=f"picked{z}{half}", align_bytes=64, offset=PICKED_AT[half])
                 else:
                     picked = keep.tile([P, HALF], U32, name=f"picked{z}{half}", align_bytes=64)
-                cols = slice(half * HALF // 16, (half + 1) * HALF // 16)
-                nc.vector.tensor_copy(picked[:], x_table[z][:].bitcast(U32).indirect(lists[:, cols]))
+                entries = slice(half * HALF // 16, (half + 1) * HALF // 16)
+                nc.vector.tensor_copy(picked[:], x_table[z][:].bitcast(U32).indirect(lists[:, entries]))
                 for part in range(HALF // CHUNK):
                     c = half * (HALF // CHUNK) + part
                     for t in range(PACK):
@@ -124,10 +115,17 @@ def tile_picked_phmlp_gelu_p_kernel(tc, x_words, x_scales, w1, w2_words, w2_scal
 
         for c in range(CHUNKS):
             h_grouped = keep.tile([P, CHUNK, PACK], BF16, name=f"h_grouped{c}", align_bytes=64)
-            nc.scalar.activation(h_grouped[:], hidden[c][:].rearrange("p t n -> p n t"), GELU)
             h_codes = keep.tile([P, CHUNK], U32, name=f"h_codes{c}", tag="h_codes", bufs=2, align_bytes=64)
             h_plane = keep.tile([P, CHUNK], U8, name=f"h_plane{c}", align_bytes=64)
-            nc.vector.quantize_mx(out=h_codes[:].bitcast(FP8X4), scales=h_plane[:], in_=h_grouped[:].rearrange("p n t -> p (n t)"))
+            pieces = 2 if c == CHUNKS - 1 else 1
+            for piece in range(pieces):
+                places = slice(piece * CHUNK // pieces, (piece + 1) * CHUNK // pieces)
+                nc.scalar.activation(h_grouped[:, places], hidden[c][:, :, places].rearrange("p t n -> p n t"), GELU)
+                nc.vector.quantize_mx(
+                    out=h_codes[:, places].bitcast(FP8X4),
+                    scales=h_plane[:, places],
+                    in_=h_grouped[:, places].rearrange("p n t -> p (n t)"),
+                )
             acc = psum.tile([N, CHUNK], F32, name=f"acc{c}", tag=f"acc{c}")
             nc.tensor.matmul_mx(
                 out=acc[:],

@@ -117,16 +117,9 @@ def tile_picked_phmlp_gelu_p_kernel(tc, x_words, x_scales, w1, w2_words, w2_scal
             h_grouped = keep.tile([P, CHUNK, PACK], BF16, name=f"h_grouped{c}", align_bytes=64)
             h_codes = keep.tile([P, CHUNK], U32, name=f"h_codes{c}", tag="h_codes", bufs=2, align_bytes=64)
             h_plane = keep.tile([P, CHUNK], U8, name=f"h_plane{c}", align_bytes=64)
-            pieces = 2 if c == CHUNKS - 1 else 1
-            for piece in range(pieces):
-                places = slice(piece * CHUNK // pieces, (piece + 1) * CHUNK // pieces)
-                nc.scalar.activation(h_grouped[:, places], hidden[c][:, :, places].rearrange("p t n -> p n t"), GELU)
-                nc.vector.quantize_mx(
-                    out=h_codes[:, places].bitcast(FP8X4),
-                    scales=h_plane[:, places],
-                    in_=h_grouped[:, places].rearrange("p n t -> p (n t)"),
-                )
-            acc = psum.tile([N, CHUNK], F32, name=f"acc{c}", tag=f"acc{c}")
+            nc.scalar.activation(h_grouped[:], hidden[c][:].rearrange("p t n -> p n t"), GELU)
+            nc.vector.quantize_mx(out=h_codes[:].bitcast(FP8X4), scales=h_plane[:], in_=h_grouped[:].rearrange("p n t -> p (n t)"))
+            acc = psum.tile([N, CHUNK], F32, name=f"acc{c}")
             nc.tensor.matmul_mx(
                 out=acc[:],
                 lhsT=w2_codes[:].bitcast(FP4X4),

@@ -23,9 +23,14 @@ HALF = 256
 CHUNK = 128
 CHUNKS = S // CHUNK
 
-SCALE_TABLE_AT = 1024
-PICKED_AT = (64, 64 + 4 * HALF)
-LAST_TABLE_AT = 64 + 2 * 4 * HALF
+FIRST_PIECE = 512
+
+RAW_BYTES = 4 * PACK * H
+SCALE_TABLE_AT = RAW_BYTES
+LAST_RAW_AT = 64
+W2_CODES_AT = SCALE_TABLE_AT + 64
+W2_PLANE_AT = W2_CODES_AT + 2 * N
+LAST_TABLE_AT = W2_PLANE_AT + N
 
 
 def tile_picked_phmlp_gelu_p_kernel(tc, x_words, x_scales, w1, w2_words, w2_scales, offs, out):
@@ -42,33 +47,38 @@ def tile_picked_phmlp_gelu_p_kernel(tc, x_words, x_scales, w1, w2_words, w2_scal
         nc.vector.memset(scale_table[:].bitcast(I32), 0)
 
         x_table = [keep.tile([P, T], I32, name="x_table0")]
-        nc.sync.dma_start(x_table[0][:], x_rows[0])
+        nc.sync.dma_start(x_table[0][:, :FIRST_PIECE], x_rows[0][:, :FIRST_PIECE])
         lists = keep.tile([P, S // 16], U16, name="lists")
         nc.sync.dma_start(lists[:], offs)
         nc.sync.dma_start(scale_table[0:P:4, :].bitcast(I32), x_scales.bitcast(I32).rearrange("z q c -> q z c"))
-        w1_raw = [keep.tile([P, PACK, H], F32, name=f"w1_raw{z}", tag=f"w1_raw{z}", align_bytes=64) for z in range(PASSES)]
-        for z in range(PASSES):
-            nc.sync.dma_start(w1_raw[z][:], w1_rows[z])
+        nc.sync.dma_start(x_table[0][:, FIRST_PIECE:], x_rows[0][:, FIRST_PIECE:])
+        w1_raw = [keep.tile([P, PACK, H], F32, name="w1_raw0", align_bytes=64)]
+        nc.sync.dma_start(w1_raw[0][:], w1_rows[0])
 
         warm_in = keep.tile([P, 1], F32, name="warm_in")
         warm_out = keep.tile([P, 1], F32, name="warm_out")
         nc.vector.memset(warm_in[:], 0.0)
         nc.scalar.activation(warm_out[:], warm_in[:], GELU)
 
-        x_planes = [keep.tile([P, S], U8, name=f"x_plane{z}", align_bytes=64) for z in range(PASSES)]
-        for z in range(PASSES):
-            nc.vector.memset(x_planes[z][:].bitcast(I32), 0)
+        x_planes = keep.tile([P, PASSES * S], U8, name="x_planes", align_bytes=64)
+        nc.vector.memset(x_planes[:].bitcast(I32), 0)
         picked_scales = keep.tile([P, S], U8, name="picked_scales", align_bytes=64)
         nc.vector.tensor_copy(picked_scales[:], scale_table[:].indirect(lists[:]))
+        for q in range(QUADRANTS):
+            nc.sync.dma_start(
+                x_planes[32 * q : 32 * q + 4, :].bitcast(I32),
+                picked_scales[32 * q : 32 * q + 32 : 4, :].bitcast(I32),
+            )
+        w1_raw.append(shared.tile([P, PACK, H], F32, name="w1_raw1", align_bytes=64, offset=LAST_RAW_AT))
+        nc.sync.dma_start(w1_raw[1][:], w1_rows[1])
         x_table.append(shared.tile([P, T], I32, name="x_table1", align_bytes=64, offset=LAST_TABLE_AT))
-        for z in range(PASSES):
-            if z == PASSES - 1:
-                nc.sync.dma_start(x_table[z][:], x_rows[z])
-            for q in range(QUADRANTS):
-                nc.sync.dma_start(
-                    x_planes[z][32 * q : 32 * q + 4, :].bitcast(I32),
-                    picked_scales[32 * q + 4 * z : 32 * q + 32 : 8, :].bitcast(I32),
-                )
+        nc.sync.dma_start(x_table[1][:], x_rows[1])
+        w2_codes = shared.tile([P, 2 * N], U8, name="w2_codes", align_bytes=64, offset=W2_CODES_AT)
+        nc.sync.dma_start(w2_codes[:].bitcast(I32), w2_words[0].bitcast(I32))
+        w2_plane = shared.tile([P, N], U8, name="w2_plane", align_bytes=64, offset=W2_PLANE_AT)
+        nc.vector.memset(w2_plane[:].bitcast(I32), 0)
+        for q in range(QUADRANTS):
+            nc.sync.dma_start(w2_plane[32 * q : 32 * q + 4, :].bitcast(I32), w2_scales[0, 4 * q : 4 * q + 4, :].bitcast(I32))
 
         w1_codes, w1_planes = {}, {}
         for z in range(PASSES):
@@ -84,20 +94,10 @@ def tile_picked_phmlp_gelu_p_kernel(tc, x_words, x_scales, w1, w2_words, w2_scal
                     w1_codes[z, 2 * pair + e] = codes[:, e * P : (e + 1) * P]
                     w1_planes[z, 2 * pair + e] = plane[:, e * P : (e + 1) * P]
 
-        w2_codes = keep.tile([P, 2 * N], U8, name="w2_codes", tag="w1_raw0", align_bytes=64)
-        nc.sync.dma_start(w2_codes[:].bitcast(I32), w2_words[0].bitcast(I32))
-        w2_plane = keep.tile([P, N], U8, name="w2_plane", tag="w1_raw1", align_bytes=64)
-        nc.vector.memset(w2_plane[:].bitcast(I32), 0)
-        for q in range(QUADRANTS):
-            nc.sync.dma_start(w2_plane[32 * q : 32 * q + 4, :].bitcast(I32), w2_scales[0, 4 * q : 4 * q + 4, :].bitcast(I32))
-
         hidden = [psum.tile([P, PACK, CHUNK], F32, name=f"hidden{c}") for c in range(CHUNKS)]
         for z in range(PASSES):
             for half in range(S // HALF):
-                if z == 0:
-                    picked = shared.tile([P, HALF], U32, name=f"picked{z}{half}", align_bytes=64, offset=PICKED_AT[half])
-                else:
-                    picked = keep.tile([P, HALF], U32, name=f"picked{z}{half}", align_bytes=64)
+                picked = keep.tile([P, HALF], U32, name=f"picked{z}{half}", align_bytes=64)
                 entries = slice(half * HALF // 16, (half + 1) * HALF // 16)
                 nc.vector.tensor_copy(picked[:], x_table[z][:].bitcast(U32).indirect(lists[:, entries]))
                 for part in range(HALF // CHUNK):
@@ -108,7 +108,7 @@ def tile_picked_phmlp_gelu_p_kernel(tc, x_words, x_scales, w1, w2_words, w2_scal
                             lhsT=w1_codes[z, t].bitcast(FP8X4),
                             lhsT_scale=w1_planes[z, t],
                             rhs=picked[:, part * CHUNK : (part + 1) * CHUNK].bitcast(FP8X4),
-                            rhs_scale=x_planes[z][:, c * CHUNK : (c + 1) * CHUNK],
+                            rhs_scale=x_planes[:, z * S + c * CHUNK : z * S + (c + 1) * CHUNK],
                             start=(z == 0 and t == 0),
                             stop=(z == PASSES - 1 and t == PACK - 1),
                         )

@@ -23,7 +23,7 @@ HALF = 256
 CHUNK = 128
 CHUNKS = S // CHUNK
 
-FIRST_PIECE = 512
+FIRST_PIECE = 768
 
 RAW_BYTES = 4 * PACK * H
 SCALE_TABLE_AT = RAW_BYTES
@@ -55,17 +55,13 @@ def tile_picked_phmlp_gelu_p_kernel(tc, x_words, x_scales, w1, w2_words, w2_scal
         w1_raw = [keep.tile([P, PACK, H], F32, name="w1_raw0", align_bytes=64)]
         nc.sync.dma_start(w1_raw[0][:], w1_rows[0])
 
-        warm_in = keep.tile([P, 1], F32, name="warm_in")
-        warm_out = keep.tile([P, 1], F32, name="warm_out")
-        nc.vector.memset(warm_in[:], 0.0)
-        nc.scalar.activation(warm_out[:], warm_in[:], GELU)
-
         x_planes = keep.tile([P, PASSES * S], U8, name="x_planes", align_bytes=64)
         nc.vector.memset(x_planes[:].bitcast(I32), 0)
         picked_scales = keep.tile([P, S], U8, name="picked_scales", align_bytes=64)
         nc.vector.tensor_copy(picked_scales[:], scale_table[:].indirect(lists[:]))
         for q in range(QUADRANTS):
-            nc.sync.dma_start(
+            queue = nc.sync if q % 2 == 0 else nc.scalar
+            queue.dma_start(
                 x_planes[32 * q : 32 * q + 4, :].bitcast(I32),
                 picked_scales[32 * q : 32 * q + 32 : 4, :].bitcast(I32),
             )
@@ -117,7 +113,11 @@ def tile_picked_phmlp_gelu_p_kernel(tc, x_words, x_scales, w1, w2_words, w2_scal
             h_grouped = keep.tile([P, CHUNK, PACK], BF16, name=f"h_grouped{c}", align_bytes=64)
             h_codes = keep.tile([P, CHUNK], U32, name=f"h_codes{c}", tag="h_codes", bufs=2, align_bytes=64)
             h_plane = keep.tile([P, CHUNK], U8, name=f"h_plane{c}", align_bytes=64)
-            nc.scalar.activation(h_grouped[:], hidden[c][:].rearrange("p t n -> p n t"), GELU)
+            nc.scalar.activation(
+                h_grouped[:].rearrange("p (n e) t -> p n t e", e=2),
+                hidden[c][:].rearrange("p t (n e) -> p n t e", e=2),
+                GELU,
+            )
             nc.vector.quantize_mx(out=h_codes[:].bitcast(FP8X4), scales=h_plane[:], in_=h_grouped[:].rearrange("p n t -> p (n t)"))
             acc = psum.tile([N, CHUNK], F32, name=f"acc{c}")
             nc.tensor.matmul_mx(

@@ -81,7 +81,7 @@ def tile_picked_phmlp_gelu_p_kernel(tc, x_words, x_scales, w1, w2_words, w2_scal
             src = w1_raw[z][:].rearrange("p j (m t) -> p m j t", t=PACK)
             for pair in range(PACK // 2):
                 grouped = keep.tile([P, 2, P, PACK], BF16, name=f"w1_grouped{z}{pair}", align_bytes=64)
-                cast = nc.vector.tensor_copy if pair == 0 else nc.scalar.copy
+                cast = nc.scalar.copy if pair == 0 else nc.vector.tensor_copy
                 cast(grouped[:].rearrange("p t m j -> p m j t"), src[:, :, :, 2 * pair : 2 * pair + 2])
                 codes = keep.tile([P, 2 * P], U32, name=f"w1_codes{z}{pair}", align_bytes=64)
                 plane = keep.tile([P, 2 * P], U8, name=f"w1_plane{z}{pair}", align_bytes=64)

@@ -59,16 +59,20 @@ def tile_picked_phmlp_gelu_p_kernel(tc, x_words, x_scales, w1, w2_words, w2_scal
         nc.vector.memset(x_planes[:].bitcast(I32), 0)
         picked_scales = keep.tile([P, S], U8, name="picked_scales", align_bytes=64)
         nc.vector.tensor_copy(picked_scales[:], scale_table[:].indirect(lists[:]))
-        for q in range(QUADRANTS):
-            queue = nc.sync if q % 2 == 0 else nc.scalar
-            queue.dma_start(
-                x_planes[32 * q : 32 * q + 4, :].bitcast(I32),
-                picked_scales[32 * q : 32 * q + 32 : 4, :].bitcast(I32),
-            )
+
+        def move_scales(z, queues):
+            for q in range(QUADRANTS):
+                queues[q % len(queues)].dma_start(
+                    x_planes[32 * q : 32 * q + 4, z * S : (z + 1) * S].bitcast(I32),
+                    picked_scales[32 * q + 4 * z : 32 * q + 32 : 8, :].bitcast(I32),
+                )
+
+        move_scales(0, [nc.sync, nc.scalar])
         w1_raw.append(shared.tile([P, PACK, H], F32, name="w1_raw1", align_bytes=64, offset=LAST_RAW_AT))
         nc.sync.dma_start(w1_raw[1][:], w1_rows[1])
         x_table.append(shared.tile([P, T], I32, name="x_table1", align_bytes=64, offset=LAST_TABLE_AT))
         nc.sync.dma_start(x_table[1][:], x_rows[1])
+        move_scales(1, [nc.sync])
         w2_codes = shared.tile([P, 2 * N], U8, name="w2_codes", align_bytes=64, offset=W2_CODES_AT)
         nc.sync.dma_start(w2_codes[:].bitcast(I32), w2_words[0].bitcast(I32))
         w2_plane = shared.tile([P, N], U8, name="w2_plane", align_bytes=64, offset=W2_PLANE_AT)

@@ -25,12 +25,13 @@ CHUNKS = S // CHUNK
 
 FIRST_PIECE = 768
 
+BURST = 256
 RAW_BYTES = 4 * PACK * H
 SCALE_TABLE_AT = RAW_BYTES
-LAST_RAW_AT = 64
-W2_CODES_AT = SCALE_TABLE_AT + 64
+LAST_RAW_AT = BURST
+W2_CODES_AT = SCALE_TABLE_AT + BURST
 W2_PLANE_AT = W2_CODES_AT + 2 * N
-LAST_TABLE_AT = W2_PLANE_AT + N
+LAST_TABLE_AT = W2_PLANE_AT + BURST
 
 
 def tile_picked_phmlp_gelu_p_kernel(tc, x_words, x_scales, w1, w2_words, w2_scales, offs, out):
@@ -43,21 +44,21 @@ def tile_picked_phmlp_gelu_p_kernel(tc, x_words, x_scales, w1, w2_words, w2_scal
         w1_rows = [w1[512 * z : 512 * (z + 1), :].rearrange("(p j) c -> p j c", j=PACK) for z in range(PASSES)]
         x_rows = [x_words[z].rearrange("p n t -> p (n t)").bitcast(I32) for z in range(PASSES)]
 
-        scale_table = shared.tile([P, T], U8, name="scale_table", align_bytes=64, offset=SCALE_TABLE_AT)
+        scale_table = shared.tile([P, T], U8, name="scale_table", align_bytes=BURST, offset=SCALE_TABLE_AT)
         nc.vector.memset(scale_table[:].bitcast(I32), 0)
 
-        x_table = [keep.tile([P, T], I32, name="x_table0")]
+        x_table = [keep.tile([P, T], I32, name="x_table0", align_bytes=BURST)]
         nc.sync.dma_start(x_table[0][:, :FIRST_PIECE], x_rows[0][:, :FIRST_PIECE])
-        lists = keep.tile([P, S // 16], U16, name="lists")
+        lists = keep.tile([P, S // 16], U16, name="lists", align_bytes=BURST)
         nc.sync.dma_start(lists[:], offs)
         nc.sync.dma_start(scale_table[0:P:4, :].bitcast(I32), x_scales.bitcast(I32).rearrange("z q c -> q z c"))
         nc.sync.dma_start(x_table[0][:, FIRST_PIECE:], x_rows[0][:, FIRST_PIECE:])
-        w1_raw = [keep.tile([P, PACK, H], F32, name="w1_raw0", align_bytes=64)]
+        w1_raw = [keep.tile([P, PACK, H], F32, name="w1_raw0", align_bytes=BURST)]
         nc.sync.dma_start(w1_raw[0][:], w1_rows[0])
 
-        x_planes = keep.tile([P, PASSES * S], U8, name="x_planes", align_bytes=64)
+        x_planes = keep.tile([P, PASSES * S], U8, name="x_planes", align_bytes=BURST)
         nc.vector.memset(x_planes[:].bitcast(I32), 0)
-        picked_scales = keep.tile([P, S], U8, name="picked_scales", align_bytes=64)
+        picked_scales = keep.tile([P, S], U8, name="picked_scales", align_bytes=BURST)
         nc.vector.tensor_copy(picked_scales[:], scale_table[:].indirect(lists[:]))
 
         def move_scales(z, queues):
@@ -68,14 +69,14 @@ def tile_picked_phmlp_gelu_p_kernel(tc, x_words, x_scales, w1, w2_words, w2_scal
                 )
 
         move_scales(0, [nc.sync, nc.scalar])
-        w1_raw.append(shared.tile([P, PACK, H], F32, name="w1_raw1", align_bytes=64, offset=LAST_RAW_AT))
+        w1_raw.append(shared.tile([P, PACK, H], F32, name="w1_raw1", align_bytes=BURST, offset=LAST_RAW_AT))
         nc.sync.dma_start(w1_raw[1][:], w1_rows[1])
-        x_table.append(shared.tile([P, T], I32, name="x_table1", align_bytes=64, offset=LAST_TABLE_AT))
+        x_table.append(shared.tile([P, T], I32, name="x_table1", align_bytes=BURST, offset=LAST_TABLE_AT))
         nc.sync.dma_start(x_table[1][:], x_rows[1])
         move_scales(1, [nc.sync])
-        w2_codes = shared.tile([P, 2 * N], U8, name="w2_codes", align_bytes=64, offset=W2_CODES_AT)
+        w2_codes = shared.tile([P, 2 * N], U8, name="w2_codes", align_bytes=BURST, offset=W2_CODES_AT)
         nc.sync.dma_start(w2_codes[:].bitcast(I32), w2_words[0].bitcast(I32))
-        w2_plane = shared.tile([P, N], U8, name="w2_plane", align_bytes=64, offset=W2_PLANE_AT)
+        w2_plane = shared.tile([P, N], U8, name="w2_plane", align_bytes=BURST, offset=W2_PLANE_AT)
         nc.vector.memset(w2_plane[:].bitcast(I32), 0)
         for q in range(QUADRANTS):
             nc.sync.dma_start(w2_plane[32 * q : 32 * q + 4, :].bitcast(I32), w2_scales[0, 4 * q : 4 * q + 4, :].bitcast(I32))
@@ -133,6 +134,6 @@ def tile_picked_phmlp_gelu_p_kernel(tc, x_words, x_scales, w1, w2_words, w2_scal
                 start=True,
                 stop=True,
             )
-            result = keep.tile([N, CHUNK], F32, name=f"result{c}")
+            result = keep.tile([N, CHUNK], F32, name=f"result{c}", align_bytes=BURST)
             nc.vector.tensor_copy(result[:], acc[:])
             nc.sync.dma_start(out[:, c * CHUNK : (c + 1) * CHUNK], result[:])

@@ -26,10 +26,8 @@ CHUNKS = S // CHUNK
 FIRST_PIECE = 768
 
 BURST = 256
-RAW_BYTES = 4 * PACK * H
-SCALE_TABLE_AT = RAW_BYTES
-LAST_RAW_AT = BURST
-W2_CODES_AT = SCALE_TABLE_AT + BURST
+LAST_PLANE_AT = 0
+W2_CODES_AT = LAST_PLANE_AT + S
 W2_PLANE_AT = W2_CODES_AT + 2 * N
 LAST_TABLE_AT = W2_PLANE_AT + BURST
 
@@ -44,42 +42,53 @@ def tile_picked_phmlp_gelu_p_kernel(tc, x_words, x_scales, w1, w2_words, w2_scal
         w1_rows = [w1[512 * z : 512 * (z + 1), :].rearrange("(p j) c -> p j c", j=PACK) for z in range(PASSES)]
         x_rows = [x_words[z].rearrange("p n t -> p (n t)").bitcast(I32) for z in range(PASSES)]
 
-        scale_table = shared.tile([P, T], U8, name="scale_table", align_bytes=BURST, offset=SCALE_TABLE_AT)
+        scale_table = keep.tile([P, T], U8, name="scale_table", align_bytes=BURST)
         nc.vector.memset(scale_table[:].bitcast(I32), 0)
 
-        x_table = [keep.tile([P, T], I32, name="x_table0", align_bytes=BURST)]
+        x_table = [shared.tile([P, T], I32, name="x_table0", align_bytes=BURST, offset=0)]
         nc.sync.dma_start(x_table[0][:, :FIRST_PIECE], x_rows[0][:, :FIRST_PIECE])
         lists = keep.tile([P, S // 16], U16, name="lists", align_bytes=BURST)
         nc.sync.dma_start(lists[:], offs)
         nc.sync.dma_start(scale_table[0:P:4, :].bitcast(I32), x_scales.bitcast(I32).rearrange("z q c -> q z c"))
         nc.sync.dma_start(x_table[0][:, FIRST_PIECE:], x_rows[0][:, FIRST_PIECE:])
-        w1_raw = [keep.tile([P, PACK, H], F32, name="w1_raw0", align_bytes=BURST)]
-        nc.sync.dma_start(w1_raw[0][:], w1_rows[0])
+        w1_raw = [keep.tile([P, PACK, H], F32, name=f"w1_raw{z}", align_bytes=BURST) for z in range(PASSES)]
+        for z in range(PASSES):
+            nc.sync.dma_start(w1_raw[z][:], w1_rows[z])
 
-        x_planes = keep.tile([P, PASSES * S], U8, name="x_planes", align_bytes=BURST)
-        nc.vector.memset(x_planes[:].bitcast(I32), 0)
+        x_planes = [keep.tile([P, S], U8, name="x_plane0", align_bytes=BURST)]
+        nc.vector.memset(x_planes[0][:].bitcast(I32), 0)
         picked_scales = keep.tile([P, S], U8, name="picked_scales", align_bytes=BURST)
         nc.vector.tensor_copy(picked_scales[:], scale_table[:].indirect(lists[:]))
 
-        def move_scales(z, queues):
+        def move_scales(z, queue):
             for q in range(QUADRANTS):
-                queues[q % len(queues)].dma_start(
-                    x_planes[32 * q : 32 * q + 4, z * S : (z + 1) * S].bitcast(I32),
+                queue.dma_start(
+                    x_planes[z][32 * q : 32 * q + 4, :].bitcast(I32),
                     picked_scales[32 * q + 4 * z : 32 * q + 32 : 8, :].bitcast(I32),
                 )
 
-        move_scales(0, [nc.sync, nc.scalar])
-        w1_raw.append(shared.tile([P, PACK, H], F32, name="w1_raw1", align_bytes=BURST, offset=LAST_RAW_AT))
-        nc.sync.dma_start(w1_raw[1][:], w1_rows[1])
+        move_scales(0, nc.scalar)
+        picked = {}
+
+        def gather_words(z):
+            for half in range(S // HALF):
+                picked[z, half] = keep.tile([P, HALF], U32, name=f"picked{z}{half}", align_bytes=64)
+                entries = slice(half * HALF // 16, (half + 1) * HALF // 16)
+                nc.vector.tensor_copy(picked[z, half][:], x_table[z][:].bitcast(U32).indirect(lists[:, entries]))
+
+        gather_words(0)
         x_table.append(shared.tile([P, T], I32, name="x_table1", align_bytes=BURST, offset=LAST_TABLE_AT))
         nc.sync.dma_start(x_table[1][:], x_rows[1])
-        move_scales(1, [nc.sync])
+        x_planes.append(shared.tile([P, S], U8, name="x_plane1", align_bytes=BURST, offset=LAST_PLANE_AT))
+        nc.vector.memset(x_planes[1][:].bitcast(I32), 0)
+        move_scales(1, nc.sync)
         w2_codes = shared.tile([P, 2 * N], U8, name="w2_codes", align_bytes=BURST, offset=W2_CODES_AT)
         nc.sync.dma_start(w2_codes[:].bitcast(I32), w2_words[0].bitcast(I32))
         w2_plane = shared.tile([P, N], U8, name="w2_plane", align_bytes=BURST, offset=W2_PLANE_AT)
         nc.vector.memset(w2_plane[:].bitcast(I32), 0)
         for q in range(QUADRANTS):
             nc.sync.dma_start(w2_plane[32 * q : 32 * q + 4, :].bitcast(I32), w2_scales[0, 4 * q : 4 * q + 4, :].bitcast(I32))
+
 
         w1_codes, w1_planes = {}, {}
         for z in range(PASSES):
@@ -96,11 +105,9 @@ def tile_picked_phmlp_gelu_p_kernel(tc, x_words, x_scales, w1, w2_words, w2_scal
                     w1_planes[z, 2 * pair + e] = plane[:, e * P : (e + 1) * P]
 
         hidden = [psum.tile([P, PACK, CHUNK], F32, name=f"hidden{c}") for c in range(CHUNKS)]
+        gather_words(1)
         for z in range(PASSES):
             for half in range(S // HALF):
-                picked = keep.tile([P, HALF], U32, name=f"picked{z}{half}", align_bytes=64)
-                entries = slice(half * HALF // 16, (half + 1) * HALF // 16)
-                nc.vector.tensor_copy(picked[:], x_table[z][:].bitcast(U32).indirect(lists[:, entries]))
                 for part in range(HALF // CHUNK):
                     c = half * (HALF // CHUNK) + part
                     for t in range(PACK):
@@ -108,8 +115,8 @@ def tile_picked_phmlp_gelu_p_kernel(tc, x_words, x_scales, w1, w2_words, w2_scal
                             out=hidden[c][:, t, :],
                             lhsT=w1_codes[z, t].bitcast(FP8X4),
                             lhsT_scale=w1_planes[z, t],
-                            rhs=picked[:, part * CHUNK : (part + 1) * CHUNK].bitcast(FP8X4),
-                            rhs_scale=x_planes[:, z * S + c * CHUNK : z * S + (c + 1) * CHUNK],
+                            rhs=picked[z, half][:, part * CHUNK : (part + 1) * CHUNK].bitcast(FP8X4),
+                            rhs_scale=x_planes[z][:, c * CHUNK : (c + 1) * CHUNK],
                             start=(z == 0 and t == 0),
                             stop=(z == PASSES - 1 and t == PACK - 1),
                         )

@@ -22,6 +22,7 @@ QUADRANTS = 4
 HALF = 256
 CHUNK = 128
 CHUNKS = S // CHUNK
+WARM_UPS = 2
 
 FIRST_PIECE = 768
 
@@ -71,10 +72,10 @@ def tile_picked_phmlp_gelu_p_kernel(tc, x_words, x_scales, w1, w2_words, w2_scal
         picked = {}
 
         def gather_words(z):
+            picked[z] = keep.tile([P, S], U32, name=f"picked{z}", align_bytes=64)
             for half in range(S // HALF):
-                picked[z, half] = keep.tile([P, HALF], U32, name=f"picked{z}{half}", align_bytes=64)
                 entries = slice(half * HALF // 16, (half + 1) * HALF // 16)
-                nc.vector.tensor_copy(picked[z, half][:], x_table[z][:].bitcast(U32).indirect(lists[:, entries]))
+                nc.vector.tensor_copy(picked[z][:, half * HALF : (half + 1) * HALF], x_table[z][:].bitcast(U32).indirect(lists[:, entries]))
 
         gather_words(0)
         x_table.append(shared.tile([P, T], I32, name="x_table1", align_bytes=BURST, offset=LAST_TABLE_AT))
@@ -106,20 +107,29 @@ def tile_picked_phmlp_gelu_p_kernel(tc, x_words, x_scales, w1, w2_words, w2_scal
 
         hidden = [psum.tile([P, PACK, CHUNK], F32, name=f"hidden{c}") for c in range(CHUNKS)]
         gather_words(1)
+        for t in range(PACK - WARM_UPS, PACK):
+            unread = psum.tile([P, S], F32, name=f"unread{t}", tag=f"acc{t}")
+            nc.tensor.matmul_mx(
+                out=unread[:],
+                lhsT=w1_codes[0, t].bitcast(FP8X4),
+                lhsT_scale=w1_planes[0, t],
+                rhs=picked[0][:].bitcast(FP8X4),
+                rhs_scale=picked_scales[:],
+                start=True,
+                stop=True,
+            )
         for z in range(PASSES):
-            for half in range(S // HALF):
-                for part in range(HALF // CHUNK):
-                    c = half * (HALF // CHUNK) + part
-                    for t in range(PACK):
-                        nc.tensor.matmul_mx(
-                            out=hidden[c][:, t, :],
-                            lhsT=w1_codes[z, t].bitcast(FP8X4),
-                            lhsT_scale=w1_planes[z, t],
-                            rhs=picked[z, half][:, part * CHUNK : (part + 1) * CHUNK].bitcast(FP8X4),
-                            rhs_scale=x_planes[z][:, c * CHUNK : (c + 1) * CHUNK],
-                            start=(z == 0 and t == 0),
-                            stop=(z == PASSES - 1 and t == PACK - 1),
-                        )
+            for c in range(CHUNKS):
+                for t in range(PACK):
+                    nc.tensor.matmul_mx(
+                        out=hidden[c][:, t, :],
+                        lhsT=w1_codes[z, t].bitcast(FP8X4),
+                        lhsT_scale=w1_planes[z, t],
+                        rhs=picked[z][:, c * CHUNK : (c + 1) * CHUNK].bitcast(FP8X4),
+                        rhs_scale=x_planes[z][:, c * CHUNK : (c + 1) * CHUNK],
+                        start=(z == 0 and t == 0),
+                        stop=(z == PASSES - 1 and t == PACK - 1),
+                    )
 
         for c in range(CHUNKS):
             h_grouped = keep.tile([P, CHUNK, PACK], BF16, name=f"h_grouped{c}", align_bytes=64)
@@ -131,7 +141,7 @@ def tile_picked_phmlp_gelu_p_kernel(tc, x_words, x_scales, w1, w2_words, w2_scal
                 GELU,
             )
             nc.vector.quantize_mx(out=h_codes[:].bitcast(FP8X4), scales=h_plane[:], in_=h_grouped[:].rearrange("p n t -> p (n t)"))
-            acc = psum.tile([N, CHUNK], F32, name=f"acc{c}")
+            acc = psum.tile([N, CHUNK], F32, name=f"acc{c}", tag=f"acc{c}")
             nc.tensor.matmul_mx(
                 out=acc[:],
                 lhsT=w2_codes[:].bitcast(FP4X4),

@@ -22,13 +22,15 @@ QUADRANTS = 4
 HALF = 256
 CHUNK = 128
 CHUNKS = S // CHUNK
-WARM_UPS = 2
+TAIL = 64
+RING = 3 * CHUNK
 
 FIRST_PIECE = 768
 
 BURST = 256
-LAST_PLANE_AT = 0
-W2_CODES_AT = LAST_PLANE_AT + S
+LAST_WEIGHTS_AT = 0
+SCALE_TABLE_AT = LAST_WEIGHTS_AT + 4 * PACK * H - BURST
+W2_CODES_AT = SCALE_TABLE_AT + BURST
 W2_PLANE_AT = W2_CODES_AT + 2 * N
 LAST_TABLE_AT = W2_PLANE_AT + BURST
 
@@ -43,32 +45,44 @@ def tile_picked_phmlp_gelu_p_kernel(tc, x_words, x_scales, w1, w2_words, w2_scal
         w1_rows = [w1[512 * z : 512 * (z + 1), :].rearrange("(p j) c -> p j c", j=PACK) for z in range(PASSES)]
         x_rows = [x_words[z].rearrange("p n t -> p (n t)").bitcast(I32) for z in range(PASSES)]
 
-        scale_table = keep.tile([P, T], U8, name="scale_table", align_bytes=BURST)
+        scale_table = shared.tile([P, T], U8, name="scale_table", align_bytes=BURST, offset=SCALE_TABLE_AT)
         nc.vector.memset(scale_table[:].bitcast(I32), 0)
 
-        x_table = [shared.tile([P, T], I32, name="x_table0", align_bytes=BURST, offset=0)]
+        x_table = [keep.tile([P, T], I32, name="x_table0", align_bytes=BURST)]
         nc.sync.dma_start(x_table[0][:, :FIRST_PIECE], x_rows[0][:, :FIRST_PIECE])
         lists = keep.tile([P, S // 16], U16, name="lists", align_bytes=BURST)
         nc.sync.dma_start(lists[:], offs)
         nc.sync.dma_start(scale_table[0:P:4, :].bitcast(I32), x_scales.bitcast(I32).rearrange("z q c -> q z c"))
         nc.sync.dma_start(x_table[0][:, FIRST_PIECE:], x_rows[0][:, FIRST_PIECE:])
-        w1_raw = [keep.tile([P, PACK, H], F32, name=f"w1_raw{z}", align_bytes=BURST) for z in range(PASSES)]
-        for z in range(PASSES):
-            nc.sync.dma_start(w1_raw[z][:], w1_rows[z])
+        w1_raw = [keep.tile([P, PACK, H], F32, name="w1_raw0", align_bytes=BURST)]
+        nc.sync.dma_start(w1_raw[0][:], w1_rows[0])
 
-        x_planes = [keep.tile([P, S], U8, name="x_plane0", align_bytes=BURST)]
-        nc.vector.memset(x_planes[0][:].bitcast(I32), 0)
+        x_planes = [keep.tile([P, S], U8, name=f"x_plane{z}", align_bytes=BURST) for z in range(PASSES)]
+        for z in range(PASSES):
+            nc.vector.memset(x_planes[z][:].bitcast(I32), 0)
         picked_scales = keep.tile([P, S], U8, name="picked_scales", align_bytes=BURST)
         nc.vector.tensor_copy(picked_scales[:], scale_table[:].indirect(lists[:]))
 
-        def move_scales(z, queue):
+        def move_scales(z, queues):
             for q in range(QUADRANTS):
-                queue.dma_start(
+                queues[q % len(queues)].dma_start(
                     x_planes[z][32 * q : 32 * q + 4, :].bitcast(I32),
                     picked_scales[32 * q + 4 * z : 32 * q + 32 : 8, :].bitcast(I32),
                 )
 
-        move_scales(0, nc.scalar)
+        move_scales(0, [nc.sync, nc.scalar])
+        w1_raw.append(shared.tile([P, PACK, H], F32, name="w1_raw1", align_bytes=BURST, offset=LAST_WEIGHTS_AT))
+        nc.sync.dma_start(w1_raw[1][:], w1_rows[1])
+        x_table.append(shared.tile([P, T], I32, name="x_table1", align_bytes=BURST, offset=LAST_TABLE_AT))
+        nc.sync.dma_start(x_table[1][:], x_rows[1])
+        move_scales(1, [nc.sync])
+        w2_codes = shared.tile([P, 2 * N], U8, name="w2_codes", align_bytes=BURST, offset=W2_CODES_AT)
+        nc.sync.dma_start(w2_codes[:].bitcast(I32), w2_words[0].bitcast(I32))
+        w2_plane = shared.tile([P, N], U8, name="w2_plane", align_bytes=BURST, offset=W2_PLANE_AT)
+        nc.vector.memset(w2_plane[:].bitcast(I32), 0)
+        for q in range(QUADRANTS):
+            nc.sync.dma_start(w2_plane[32 * q : 32 * q + 4, :].bitcast(I32), w2_scales[0, 4 * q : 4 * q + 4, :].bitcast(I32))
+
         picked = {}
 
         def gather_words(z):
@@ -78,79 +92,96 @@ def tile_picked_phmlp_gelu_p_kernel(tc, x_words, x_scales, w1, w2_words, w2_scal
                 nc.vector.tensor_copy(picked[z][:, half * HALF : (half + 1) * HALF], x_table[z][:].bitcast(U32).indirect(lists[:, entries]))
 
         gather_words(0)
-        x_table.append(shared.tile([P, T], I32, name="x_table1", align_bytes=BURST, offset=LAST_TABLE_AT))
-        nc.sync.dma_start(x_table[1][:], x_rows[1])
-        x_planes.append(shared.tile([P, S], U8, name="x_plane1", align_bytes=BURST, offset=LAST_PLANE_AT))
-        nc.vector.memset(x_planes[1][:].bitcast(I32), 0)
-        move_scales(1, nc.sync)
-        w2_codes = shared.tile([P, 2 * N], U8, name="w2_codes", align_bytes=BURST, offset=W2_CODES_AT)
-        nc.sync.dma_start(w2_codes[:].bitcast(I32), w2_words[0].bitcast(I32))
-        w2_plane = shared.tile([P, N], U8, name="w2_plane", align_bytes=BURST, offset=W2_PLANE_AT)
-        nc.vector.memset(w2_plane[:].bitcast(I32), 0)
-        for q in range(QUADRANTS):
-            nc.sync.dma_start(w2_plane[32 * q : 32 * q + 4, :].bitcast(I32), w2_scales[0, 4 * q : 4 * q + 4, :].bitcast(I32))
-
 
         w1_codes, w1_planes = {}, {}
         for z in range(PASSES):
             src = w1_raw[z][:].rearrange("p j (m t) -> p m j t", t=PACK)
-            for pair in range(PACK // 2):
-                grouped = keep.tile([P, 2, P, PACK], BF16, name=f"w1_grouped{z}{pair}", align_bytes=64)
-                cast = nc.scalar.copy if pair == 0 else nc.vector.tensor_copy
-                cast(grouped[:].rearrange("p t m j -> p m j t"), src[:, :, :, 2 * pair : 2 * pair + 2])
-                codes = keep.tile([P, 2 * P], U32, name=f"w1_codes{z}{pair}", align_bytes=64)
-                plane = keep.tile([P, 2 * P], U8, name=f"w1_plane{z}{pair}", align_bytes=64)
-                nc.vector.quantize_mx(out=codes[:].bitcast(FP8X4), scales=plane[:], in_=grouped[:].rearrange("p t m j -> p (t m j)"))
-                for e in range(2):
-                    w1_codes[z, 2 * pair + e] = codes[:, e * P : (e + 1) * P]
-                    w1_planes[z, 2 * pair + e] = plane[:, e * P : (e + 1) * P]
+            grouped = keep.tile([P, PACK, P, PACK], BF16, name=f"w1_grouped{z}", align_bytes=64)
+            codes = keep.tile([P, PACK * P], U32, name=f"w1_codes{z}", align_bytes=64)
+            plane = keep.tile([P, PACK * P], U8, name=f"w1_plane{z}", align_bytes=64)
+            for pair, cast in enumerate([nc.scalar.copy, nc.vector.tensor_copy]):
+                cast(grouped[:, 2 * pair : 2 * pair + 2].rearrange("p t m j -> p m j t"), src[:, :, :, 2 * pair : 2 * pair + 2])
+            for tiles in [range(PACK)] if z == 0 else [range(2, 4), range(0, 2)]:
+                cols = slice(tiles.start * P, tiles.stop * P)
+                nc.vector.quantize_mx(
+                    out=codes[:, cols].bitcast(FP8X4),
+                    scales=plane[:, cols],
+                    in_=grouped[:, tiles.start : tiles.stop].rearrange("p t m j -> p (t m j)"),
+                )
+            for t in range(PACK):
+                w1_codes[z, t] = codes[:, t * P : (t + 1) * P]
+                w1_planes[z, t] = plane[:, t * P : (t + 1) * P]
 
-        hidden = [psum.tile([P, PACK, CHUNK], F32, name=f"hidden{c}") for c in range(CHUNKS)]
+        banks = [(0, range(0, 2)), (0, range(2, 4))] + [(c, range(PACK)) for c in range(1, CHUNKS)]
+        hidden = [psum.tile([P, len(tiles), CHUNK], F32, name=f"hidden{b}", tag=f"hidden{b}") for b, (c, tiles) in enumerate(banks)]
         gather_words(1)
-        for t in range(PACK - WARM_UPS, PACK):
-            unread = psum.tile([P, S], F32, name=f"unread{t}", tag=f"acc{t}")
-            nc.tensor.matmul_mx(
-                out=unread[:],
-                lhsT=w1_codes[0, t].bitcast(FP8X4),
-                lhsT_scale=w1_planes[0, t],
-                rhs=picked[0][:].bitcast(FP8X4),
-                rhs_scale=picked_scales[:],
-                start=True,
-                stop=True,
-            )
         for z in range(PASSES):
-            for c in range(CHUNKS):
-                for t in range(PACK):
+            for b, (c, tiles) in enumerate(banks):
+                for t in tiles:
                     nc.tensor.matmul_mx(
-                        out=hidden[c][:, t, :],
+                        out=hidden[b][:, t - tiles[0], :],
                         lhsT=w1_codes[z, t].bitcast(FP8X4),
                         lhsT_scale=w1_planes[z, t],
                         rhs=picked[z][:, c * CHUNK : (c + 1) * CHUNK].bitcast(FP8X4),
                         rhs_scale=x_planes[z][:, c * CHUNK : (c + 1) * CHUNK],
-                        start=(z == 0 and t == 0),
-                        stop=(z == PASSES - 1 and t == PACK - 1),
+                        start=(z == 0 and t == tiles[0]),
+                        stop=(z == PASSES - 1 and t == tiles[-1]),
                     )
 
-        for c in range(CHUNKS):
-            h_grouped = keep.tile([P, CHUNK, PACK], BF16, name=f"h_grouped{c}", align_bytes=64)
-            h_codes = keep.tile([P, CHUNK], U32, name=f"h_codes{c}", tag="h_codes", bufs=2, align_bytes=64)
-            h_plane = keep.tile([P, CHUNK], U8, name=f"h_plane{c}", align_bytes=64)
+        def gelu(dst, bank):
             nc.scalar.activation(
-                h_grouped[:].rearrange("p (n e) t -> p n t e", e=2),
-                hidden[c][:].rearrange("p t (n e) -> p n t e", e=2),
+                dst.rearrange("p (n e) t -> p n t e", e=2),
+                bank.rearrange("p t (n e) -> p n t e", e=2),
                 GELU,
             )
-            nc.vector.quantize_mx(out=h_codes[:].bitcast(FP8X4), scales=h_plane[:], in_=h_grouped[:].rearrange("p n t -> p (n t)"))
-            acc = psum.tile([N, CHUNK], F32, name=f"acc{c}", tag=f"acc{c}")
+
+        pieces = [(c * CHUNK, (c + 1) * CHUNK) for c in range(CHUNKS - 1)] + [(S - CHUNK, S - TAIL), (S - TAIL, S)]
+        h_pairs = keep.tile([P, 2, CHUNK, 2], BF16, name="h_pairs", align_bytes=64)
+        h_codes = keep.tile([P, RING], U32, name="h_codes", align_bytes=64)
+        h_plane = keep.tile([P, RING], U8, name="h_plane", align_bytes=64)
+        spare_banks = ["spare0", "spare1", "spare2", "hidden0", "hidden1"]
+        stores = [[0], [1], [2], [3, 4]]
+        acc = {}
+
+        def product(n):
+            lo, hi = pieces[n]
+            c = lo // CHUNK
+            h_grouped = keep.tile([P, hi - lo, PACK], BF16, name=f"h_grouped{n}", align_bytes=64)
+            if c == 0:
+                for u in range(2):
+                    gelu(h_pairs[:, u], hidden[u][:])
+                nc.vector.tensor_copy(h_grouped[:].rearrange("p n (u e) -> p n u e", e=2), h_pairs[:].rearrange("p u n e -> p n u e"))
+            else:
+                gelu(h_grouped[:], hidden[c + 1][:, :, lo - c * CHUNK : hi - c * CHUNK])
+            end = (hi - CHUNK - 1) % RING + 1
+            made, read = slice(end - (hi - lo), end), slice(end - CHUNK, end)
+            nc.vector.quantize_mx(out=h_codes[:, made].bitcast(FP8X4), scales=h_plane[:, made], in_=h_grouped[:].rearrange("p n t -> p (n t)"))
+            acc[n] = psum.tile([N, CHUNK], F32, name=f"acc{n}", tag=spare_banks[n])
             nc.tensor.matmul_mx(
-                out=acc[:],
+                out=acc[n][:],
                 lhsT=w2_codes[:].bitcast(FP4X4),
                 lhsT_scale=w2_plane[:],
-                rhs=h_codes[:].bitcast(FP8X4),
-                rhs_scale=h_plane[:],
+                rhs=h_codes[:, read].bitcast(FP8X4),
+                rhs_scale=h_plane[:, read],
                 start=True,
                 stop=True,
             )
-            result = keep.tile([N, CHUNK], F32, name=f"result{c}", align_bytes=BURST)
-            nc.vector.tensor_copy(result[:], acc[:])
-            nc.sync.dma_start(out[:, c * CHUNK : (c + 1) * CHUNK], result[:])
+
+        def store(group):
+            first, last = pieces[group[0]][0], pieces[group[-1]][1]
+            result = keep.tile([N, last - first], F32, name=f"result{group[0]}", align_bytes=BURST)
+            for n in group:
+                copy = nc.vector.tensor_copy if n in (0, 3, 4) else nc.scalar.copy
+                lo, hi = pieces[n]
+                copy(result[:, lo - first : hi - first], acc[n][:, CHUNK - (hi - lo) :])
+            nc.sync.dma_start(out[:, first:last], result[:])
+
+        product(0)
+        product(1)
+        product(2)
+        store(stores[0])
+        product(3)
+        product(4)
+        store(stores[1])
+        store(stores[2])
+        store(stores[3])

@@ -19,6 +19,7 @@ P = 128
 PACK = 4
 PASSES = K // (P * PACK)
 QUADRANTS = 4
+ROWS = 4
 HALF = 256
 CHUNK = 128
 CHUNKS = S // CHUNK
@@ -64,10 +65,10 @@ def tile_picked_phmlp_gelu_p_kernel(tc, x_words, x_scales, w1, w2_words, w2_scal
         nc.vector.tensor_copy(picked_scales[:], scale_table[:].indirect(lists[:]))
 
         def move_scales(z, queues):
-            for q in range(QUADRANTS):
-                queues[q % len(queues)].dma_start(
-                    x_planes[z][32 * q : 32 * q + 4, :].bitcast(I32),
-                    picked_scales[32 * q + 4 * z : 32 * q + 32 : 8, :].bitcast(I32),
+            for i in range(ROWS):
+                queues[i % len(queues)].dma_start(
+                    x_planes[z][i:P:32, :].bitcast(I32),
+                    picked_scales[8 * i + 4 * z : P : 32, :].bitcast(I32),
                 )
 
         move_scales(0, [nc.sync, nc.scalar])
@@ -112,7 +113,7 @@ def tile_picked_phmlp_gelu_p_kernel(tc, x_words, x_scales, w1, w2_words, w2_scal
                 w1_codes[z, t] = codes[:, t * P : (t + 1) * P]
                 w1_planes[z, t] = plane[:, t * P : (t + 1) * P]
 
-        banks = [(0, range(0, 2)), (0, range(2, 4))] + [(c, range(PACK)) for c in range(1, CHUNKS)]
+        banks = [(0, range(0, 1)), (0, range(1, 2)), (0, range(2, 4))] + [(c, range(PACK)) for c in range(1, CHUNKS)]
         hidden = [psum.tile([P, len(tiles), CHUNK], F32, name=f"hidden{b}", tag=f"hidden{b}") for b, (c, tiles) in enumerate(banks)]
         gather_words(1)
         for z in range(PASSES):
@@ -136,10 +137,10 @@ def tile_picked_phmlp_gelu_p_kernel(tc, x_words, x_scales, w1, w2_words, w2_scal
             )
 
         pieces = [(c * CHUNK, (c + 1) * CHUNK) for c in range(CHUNKS - 1)] + [(S - CHUNK, S - TAIL), (S - TAIL, S)]
-        h_pairs = keep.tile([P, 2, CHUNK, 2], BF16, name="h_pairs", align_bytes=64)
+        h_tiles = keep.tile([P, PACK, CHUNK], BF16, name="h_tiles", align_bytes=64)
         h_codes = keep.tile([P, RING], U32, name="h_codes", align_bytes=64)
         h_plane = keep.tile([P, RING], U8, name="h_plane", align_bytes=64)
-        spare_banks = ["spare0", "spare1", "spare2", "hidden0", "hidden1"]
+        spare_banks = ["spare0", "spare1", "hidden0", "hidden1", "hidden2"]
         stores = [[0], [1], [2], [3, 4]]
         acc = {}
 
@@ -148,11 +149,14 @@ def tile_picked_phmlp_gelu_p_kernel(tc, x_words, x_scales, w1, w2_words, w2_scal
             c = lo // CHUNK
             h_grouped = keep.tile([P, hi - lo, PACK], BF16, name=f"h_grouped{n}", align_bytes=64)
             if c == 0:
-                for u in range(2):
-                    gelu(h_pairs[:, u], hidden[u][:])
-                nc.vector.tensor_copy(h_grouped[:].rearrange("p n (u e) -> p n u e", e=2), h_pairs[:].rearrange("p u n e -> p n u e"))
+                for b in range(3):
+                    tiles = banks[b][1]
+                    nc.scalar.activation(h_tiles[:, tiles.start : tiles.stop], hidden[b][:], GELU)
+                nc.vector.tensor_copy(
+                    h_grouped[:].rearrange("p (n e) t -> p n t e", e=PACK), h_tiles[:].rearrange("p t (n e) -> p n t e", e=PACK)
+                )
             else:
-                gelu(h_grouped[:], hidden[c + 1][:, :, lo - c * CHUNK : hi - c * CHUNK])
+                gelu(h_grouped[:], hidden[c + 2][:, :, lo - c * CHUNK : hi - c * CHUNK])
             end = (hi - CHUNK - 1) % RING + 1
             made, read = slice(end - (hi - lo), end), slice(end - CHUNK, end)
             nc.vector.quantize_mx(out=h_codes[:, made].bitcast(FP8X4), scales=h_plane[:, made], in_=h_grouped[:].rearrange("p n t -> p (n t)"))

@@ -24,7 +24,7 @@ HALF = 256
 CHUNK = 128
 CHUNKS = S // CHUNK
 TAIL = 64
-RING = 3 * CHUNK
+RING = 2 * CHUNK
 
 FIRST_PIECE = 768
 
@@ -141,32 +141,41 @@ def tile_picked_phmlp_gelu_p_kernel(tc, x_words, x_scales, w1, w2_words, w2_scal
         h_codes = keep.tile([P, RING], U32, name="h_codes", align_bytes=64)
         h_plane = keep.tile([P, RING], U8, name="h_plane", align_bytes=64)
         spare_banks = ["spare0", "spare1", "hidden0", "hidden1", "hidden2"]
-        stores = [[0], [1], [2], [3, 4]]
-        acc = {}
+        stores = [[1], [0], [2], [3, 4]]
+        h_grouped, acc = {}, {}
 
-        def product(n):
+        def activate(n):
             lo, hi = pieces[n]
             c = lo // CHUNK
-            h_grouped = keep.tile([P, hi - lo, PACK], BF16, name=f"h_grouped{n}", align_bytes=64)
+            h_grouped[n] = keep.tile([P, hi - lo, PACK], BF16, name=f"h_grouped{n}", tag=f"h_grouped{n}", align_bytes=64)
             if c == 0:
                 for b in range(3):
                     tiles = banks[b][1]
                     nc.scalar.activation(h_tiles[:, tiles.start : tiles.stop], hidden[b][:], GELU)
                 nc.vector.tensor_copy(
-                    h_grouped[:].rearrange("p (n e) t -> p n t e", e=PACK), h_tiles[:].rearrange("p t (n e) -> p n t e", e=PACK)
+                    h_grouped[n][:].rearrange("p (n e) t -> p n t e", e=PACK), h_tiles[:].rearrange("p t (n e) -> p n t e", e=PACK)
                 )
             else:
-                gelu(h_grouped[:], hidden[c + 2][:, :, lo - c * CHUNK : hi - c * CHUNK])
-            end = (hi - CHUNK - 1) % RING + 1
+                gelu(h_grouped[n][:], hidden[c + 2][:, :, lo - c * CHUNK : hi - c * CHUNK])
+
+        def product(n):
+            lo, hi = pieces[n]
+            if n == 0:
+                codes = keep.tile([P, CHUNK], U32, name="h_codes0", tag="h_grouped1", align_bytes=64)
+                plane = keep.tile([P, CHUNK], U8, name="h_plane0", align_bytes=64)
+                end = CHUNK
+            else:
+                codes, plane = h_codes, h_plane
+                end = (hi - 1) % RING + 1
             made, read = slice(end - (hi - lo), end), slice(end - CHUNK, end)
-            nc.vector.quantize_mx(out=h_codes[:, made].bitcast(FP8X4), scales=h_plane[:, made], in_=h_grouped[:].rearrange("p n t -> p (n t)"))
+            nc.vector.quantize_mx(out=codes[:, made].bitcast(FP8X4), scales=plane[:, made], in_=h_grouped[n][:].rearrange("p n t -> p (n t)"))
             acc[n] = psum.tile([N, CHUNK], F32, name=f"acc{n}", tag=spare_banks[n])
             nc.tensor.matmul_mx(
                 out=acc[n][:],
                 lhsT=w2_codes[:].bitcast(FP4X4),
                 lhsT_scale=w2_plane[:],
-                rhs=h_codes[:, read].bitcast(FP8X4),
-                rhs_scale=h_plane[:, read],
+                rhs=codes[:, read].bitcast(FP8X4),
+                rhs_scale=plane[:, read],
                 start=True,
                 stop=True,
             )
@@ -175,13 +184,15 @@ def tile_picked_phmlp_gelu_p_kernel(tc, x_words, x_scales, w1, w2_words, w2_scal
             first, last = pieces[group[0]][0], pieces[group[-1]][1]
             result = keep.tile([N, last - first], F32, name=f"result{group[0]}", align_bytes=BURST)
             for n in group:
-                copy = nc.vector.tensor_copy if n in (0, 3, 4) else nc.scalar.copy
+                copy = nc.vector.tensor_copy if n in (1, 3, 4) else nc.scalar.copy
                 lo, hi = pieces[n]
                 copy(result[:, lo - first : hi - first], acc[n][:, CHUNK - (hi - lo) :])
             nc.sync.dma_start(out[:, first:last], result[:])
 
-        product(0)
+        for n in range(len(pieces)):
+            activate(n)
         product(1)
+        product(0)
         product(2)
         store(stores[0])
         product(3)

@@ -26,14 +26,16 @@ CHUNKS = S // CHUNK
 TAIL = 64
 RING = 2 * CHUNK
 
-FIRST_PIECE = 768
+FIRST_PIECE = 640
 
 BURST = 256
 LAST_WEIGHTS_AT = 0
-SCALE_TABLE_AT = LAST_WEIGHTS_AT + 4 * PACK * H - BURST
-W2_CODES_AT = SCALE_TABLE_AT + BURST
+FIRST_PICKED_AT = LAST_WEIGHTS_AT + 4 * PACK * H
+PICKED_SCALES_AT = FIRST_PICKED_AT - BURST
+FIRST_TABLE_AT = FIRST_PICKED_AT + 4 * S
+W2_CODES_AT = FIRST_TABLE_AT
 W2_PLANE_AT = W2_CODES_AT + 2 * N
-LAST_TABLE_AT = W2_PLANE_AT + BURST
+LAST_TABLE_AT = FIRST_TABLE_AT + 4 * T - BURST
 
 
 def tile_picked_phmlp_gelu_p_kernel(tc, x_words, x_scales, w1, w2_words, w2_scales, offs, out):
@@ -46,10 +48,10 @@ def tile_picked_phmlp_gelu_p_kernel(tc, x_words, x_scales, w1, w2_words, w2_scal
         w1_rows = [w1[512 * z : 512 * (z + 1), :].rearrange("(p j) c -> p j c", j=PACK) for z in range(PASSES)]
         x_rows = [x_words[z].rearrange("p n t -> p (n t)").bitcast(I32) for z in range(PASSES)]
 
-        scale_table = shared.tile([P, T], U8, name="scale_table", align_bytes=BURST, offset=SCALE_TABLE_AT)
+        scale_table = keep.tile([P, T], U8, name="scale_table", align_bytes=BURST)
         nc.vector.memset(scale_table[:].bitcast(I32), 0)
 
-        x_table = [keep.tile([P, T], I32, name="x_table0", align_bytes=BURST)]
+        x_table = [shared.tile([P, T], I32, name="x_table0", align_bytes=BURST, offset=FIRST_TABLE_AT)]
         nc.sync.dma_start(x_table[0][:, :FIRST_PIECE], x_rows[0][:, :FIRST_PIECE])
         lists = keep.tile([P, S // 16], U16, name="lists", align_bytes=BURST)
         nc.sync.dma_start(lists[:], offs)
@@ -59,23 +61,36 @@ def tile_picked_phmlp_gelu_p_kernel(tc, x_words, x_scales, w1, w2_words, w2_scal
         nc.sync.dma_start(w1_raw[0][:], w1_rows[0])
 
         x_planes = [keep.tile([P, S], U8, name=f"x_plane{z}", align_bytes=BURST) for z in range(PASSES)]
-        for z in range(PASSES):
-            nc.vector.memset(x_planes[z][:].bitcast(I32), 0)
-        picked_scales = keep.tile([P, S], U8, name="picked_scales", align_bytes=BURST)
+        picked_scales = shared.tile([P, S], U8, name="picked_scales", align_bytes=BURST, offset=PICKED_SCALES_AT)
         nc.vector.tensor_copy(picked_scales[:], scale_table[:].indirect(lists[:]))
+        nc.vector.tensor_copy(x_planes[0][:].bitcast(I32), picked_scales[:].bitcast(I32))
 
         def move_scales(z, queues):
-            for i in range(ROWS):
+            for i in range(1, ROWS):
                 queues[i % len(queues)].dma_start(
-                    x_planes[z][i:P:32, :].bitcast(I32),
-                    picked_scales[8 * i + 4 * z : P : 32, :].bitcast(I32),
+                    x_planes[z][4 * z + i : P : 32, :].bitcast(I32),
+                    x_planes[z][8 * i + 4 * z : P : 32, :].bitcast(I32),
                 )
 
-        move_scales(0, [nc.sync, nc.scalar])
+        move_scales(0, [nc.scalar, nc.sync])
         w1_raw.append(shared.tile([P, PACK, H], F32, name="w1_raw1", align_bytes=BURST, offset=LAST_WEIGHTS_AT))
         nc.sync.dma_start(w1_raw[1][:], w1_rows[1])
+
+        picked = {}
+
+        def gather_words(z):
+            if z == 0:
+                picked[z] = shared.tile([P, S], U32, name="picked0", align_bytes=BURST, offset=FIRST_PICKED_AT)
+            else:
+                picked[z] = keep.tile([P, S], U32, name="picked1", align_bytes=64)
+            for half in range(S // HALF):
+                entries = slice(half * HALF // 16, (half + 1) * HALF // 16)
+                nc.vector.tensor_copy(picked[z][:, half * HALF : (half + 1) * HALF], x_table[z][:].bitcast(U32).indirect(lists[:, entries]))
+
+        gather_words(0)
         x_table.append(shared.tile([P, T], I32, name="x_table1", align_bytes=BURST, offset=LAST_TABLE_AT))
         nc.sync.dma_start(x_table[1][:], x_rows[1])
+        nc.vector.tensor_copy(x_planes[1][:].bitcast(I32), x_planes[0][:].bitcast(I32))
         move_scales(1, [nc.sync])
         w2_codes = shared.tile([P, 2 * N], U8, name="w2_codes", align_bytes=BURST, offset=W2_CODES_AT)
         nc.sync.dma_start(w2_codes[:].bitcast(I32), w2_words[0].bitcast(I32))
@@ -83,16 +98,6 @@ def tile_picked_phmlp_gelu_p_kernel(tc, x_words, x_scales, w1, w2_words, w2_scal
         nc.vector.memset(w2_plane[:].bitcast(I32), 0)
         for q in range(QUADRANTS):
             nc.sync.dma_start(w2_plane[32 * q : 32 * q + 4, :].bitcast(I32), w2_scales[0, 4 * q : 4 * q + 4, :].bitcast(I32))
-
-        picked = {}
-
-        def gather_words(z):
-            picked[z] = keep.tile([P, S], U32, name=f"picked{z}", align_bytes=64)
-            for half in range(S // HALF):
-                entries = slice(half * HALF // 16, (half + 1) * HALF // 16)
-                nc.vector.tensor_copy(picked[z][:, half * HALF : (half + 1) * HALF], x_table[z][:].bitcast(U32).indirect(lists[:, entries]))
-
-        gather_words(0)
 
         w1_codes, w1_planes = {}, {}
         for z in range(PASSES):
@@ -124,7 +129,7 @@ def tile_picked_phmlp_gelu_p_kernel(tc, x_words, x_scales, w1, w2_words, w2_scal
                         lhsT=w1_codes[z, t].bitcast(FP8X4),
                         lhsT_scale=w1_planes[z, t],
                         rhs=picked[z][:, c * CHUNK : (c + 1) * CHUNK].bitcast(FP8X4),
-                        rhs_scale=x_planes[z][:, c * CHUNK : (c + 1) * CHUNK],
+                        rhs_scale=x_planes[z][4 * z :, c * CHUNK : (c + 1) * CHUNK],
                         start=(z == 0 and t == tiles[0]),
                         stop=(z == PASSES - 1 and t == tiles[-1]),
                     )

@@ -26,7 +26,7 @@ CHUNKS = S // CHUNK
 TAIL = 64
 RING = 2 * CHUNK
 
-FIRST_PIECE = 640
+FIRST_PIECE = 384
 
 BURST = 256
 LAST_WEIGHTS_AT = 0

@@ -26,16 +26,15 @@ CHUNKS = S // CHUNK
 TAIL = 64
 RING = 2 * CHUNK
 
-FIRST_PIECE = 384
+EARLY_ROWS = 2
 
 BURST = 256
 LAST_WEIGHTS_AT = 0
-FIRST_PICKED_AT = LAST_WEIGHTS_AT + 4 * PACK * H
-PICKED_SCALES_AT = FIRST_PICKED_AT - BURST
-FIRST_TABLE_AT = FIRST_PICKED_AT + 4 * S
-W2_CODES_AT = FIRST_TABLE_AT
+LAST_TABLE_AT = LAST_WEIGHTS_AT + 4 * (PACK - EARLY_ROWS) * H
+PICKED_SCALES_AT = LAST_TABLE_AT - BURST
+FIRST_WEIGHTS_AT = LAST_TABLE_AT + 4 * T
+W2_CODES_AT = FIRST_WEIGHTS_AT
 W2_PLANE_AT = W2_CODES_AT + 2 * N
-LAST_TABLE_AT = FIRST_TABLE_AT + 4 * T - BURST
 
 
 def tile_picked_phmlp_gelu_p_kernel(tc, x_words, x_scales, w1, w2_words, w2_scales, offs, out):
@@ -51,62 +50,57 @@ def tile_picked_phmlp_gelu_p_kernel(tc, x_words, x_scales, w1, w2_words, w2_scal
         scale_table = keep.tile([P, T], U8, name="scale_table", align_bytes=BURST)
         nc.vector.memset(scale_table[:].bitcast(I32), 0)
 
-        x_table = [shared.tile([P, T], I32, name="x_table0", align_bytes=BURST, offset=FIRST_TABLE_AT)]
-        nc.sync.dma_start(x_table[0][:, :FIRST_PIECE], x_rows[0][:, :FIRST_PIECE])
+        w1_early = keep.tile([P, EARLY_ROWS, H], F32, name="w1_early", align_bytes=BURST)
+        nc.sync.dma_start(w1_early[:], w1_rows[1][:, :EARLY_ROWS])
         lists = keep.tile([P, S // 16], U16, name="lists", align_bytes=BURST)
         nc.sync.dma_start(lists[:], offs)
         nc.sync.dma_start(scale_table[0:P:4, :].bitcast(I32), x_scales.bitcast(I32).rearrange("z q c -> q z c"))
-        nc.sync.dma_start(x_table[0][:, FIRST_PIECE:], x_rows[0][:, FIRST_PIECE:])
-        w1_raw = [keep.tile([P, PACK, H], F32, name="w1_raw0", align_bytes=BURST)]
-        nc.sync.dma_start(w1_raw[0][:], w1_rows[0])
+        w1_first = shared.tile([P, PACK, H], F32, name="w1_first", align_bytes=BURST, offset=FIRST_WEIGHTS_AT)
+        nc.sync.dma_start(w1_first[:], w1_rows[0])
+        x_table = [keep.tile([P, T], I32, name="x_table0", align_bytes=BURST)]
+        nc.sync.dma_start(x_table[0][:], x_rows[0])
 
         x_planes = [keep.tile([P, S], U8, name=f"x_plane{z}", align_bytes=BURST) for z in range(PASSES)]
         picked_scales = shared.tile([P, S], U8, name="picked_scales", align_bytes=BURST, offset=PICKED_SCALES_AT)
         nc.vector.tensor_copy(picked_scales[:], scale_table[:].indirect(lists[:]))
-        nc.vector.tensor_copy(x_planes[0][:].bitcast(I32), picked_scales[:].bitcast(I32))
+        for z in range(PASSES):
+            nc.vector.tensor_copy(x_planes[z][:].bitcast(I32), picked_scales[:].bitcast(I32))
 
-        def move_scales(z, queues):
+        def move_scales(z):
             for i in range(1, ROWS):
-                queues[i % len(queues)].dma_start(
+                nc.sync.dma_start(
                     x_planes[z][4 * z + i : P : 32, :].bitcast(I32),
                     x_planes[z][8 * i + 4 * z : P : 32, :].bitcast(I32),
                 )
 
-        move_scales(0, [nc.scalar, nc.sync])
-        w1_raw.append(shared.tile([P, PACK, H], F32, name="w1_raw1", align_bytes=BURST, offset=LAST_WEIGHTS_AT))
-        nc.sync.dma_start(w1_raw[1][:], w1_rows[1])
+        move_scales(0)
+        w1_late = shared.tile([P, PACK - EARLY_ROWS, H], F32, name="w1_late", align_bytes=BURST, offset=LAST_WEIGHTS_AT)
+        nc.sync.dma_start(w1_late[:], w1_rows[1][:, EARLY_ROWS:])
+        x_table.append(shared.tile([P, T], I32, name="x_table1", align_bytes=BURST, offset=LAST_TABLE_AT))
+        nc.sync.dma_start(x_table[1][:], x_rows[1])
+        move_scales(1)
 
-        picked = {}
+        picked = [keep.tile([P, S], U32, name=f"picked{z}", align_bytes=64) for z in range(PASSES)]
 
         def gather_words(z):
-            if z == 0:
-                picked[z] = shared.tile([P, S], U32, name="picked0", align_bytes=BURST, offset=FIRST_PICKED_AT)
-            else:
-                picked[z] = keep.tile([P, S], U32, name="picked1", align_bytes=64)
             for half in range(S // HALF):
                 entries = slice(half * HALF // 16, (half + 1) * HALF // 16)
                 nc.vector.tensor_copy(picked[z][:, half * HALF : (half + 1) * HALF], x_table[z][:].bitcast(U32).indirect(lists[:, entries]))
 
-        gather_words(0)
-        x_table.append(shared.tile([P, T], I32, name="x_table1", align_bytes=BURST, offset=LAST_TABLE_AT))
-        nc.sync.dma_start(x_table[1][:], x_rows[1])
-        nc.vector.tensor_copy(x_planes[1][:].bitcast(I32), x_planes[0][:].bitcast(I32))
-        move_scales(1, [nc.sync])
-        w2_codes = shared.tile([P, 2 * N], U8, name="w2_codes", align_bytes=BURST, offset=W2_CODES_AT)
-        nc.sync.dma_start(w2_codes[:].bitcast(I32), w2_words[0].bitcast(I32))
-        w2_plane = shared.tile([P, N], U8, name="w2_plane", align_bytes=BURST, offset=W2_PLANE_AT)
-        nc.vector.memset(w2_plane[:].bitcast(I32), 0)
-        for q in range(QUADRANTS):
-            nc.sync.dma_start(w2_plane[32 * q : 32 * q + 4, :].bitcast(I32), w2_scales[0, 4 * q : 4 * q + 4, :].bitcast(I32))
-
+        both = [nc.scalar.copy, nc.vector.tensor_copy]
+        parts = [
+            [(w1_first, slice(0, PACK), both)],
+            [(w1_early, slice(0, EARLY_ROWS), [nc.scalar.copy] * 2), (w1_late, slice(EARLY_ROWS, PACK), both)],
+        ]
         w1_codes, w1_planes = {}, {}
         for z in range(PASSES):
-            src = w1_raw[z][:].rearrange("p j (m t) -> p m j t", t=PACK)
             grouped = keep.tile([P, PACK, P, PACK], BF16, name=f"w1_grouped{z}", align_bytes=64)
             codes = keep.tile([P, PACK * P], U32, name=f"w1_codes{z}", align_bytes=64)
             plane = keep.tile([P, PACK * P], U8, name=f"w1_plane{z}", align_bytes=64)
-            for pair, cast in enumerate([nc.scalar.copy, nc.vector.tensor_copy]):
-                cast(grouped[:, 2 * pair : 2 * pair + 2].rearrange("p t m j -> p m j t"), src[:, :, :, 2 * pair : 2 * pair + 2])
+            for raw, rows, casts in parts[z]:
+                src = raw[:].rearrange("p j (m t) -> p m j t", t=PACK)
+                for pair, cast in enumerate(casts):
+                    cast(grouped[:, 2 * pair : 2 * pair + 2, :, rows].rearrange("p t m j -> p m j t"), src[:, :, :, 2 * pair : 2 * pair + 2])
             for tiles in [range(PACK)] if z == 0 else [range(2, 4), range(0, 2)]:
                 cols = slice(tiles.start * P, tiles.stop * P)
                 nc.vector.quantize_mx(
@@ -117,6 +111,15 @@ def tile_picked_phmlp_gelu_p_kernel(tc, x_words, x_scales, w1, w2_words, w2_scal
             for t in range(PACK):
                 w1_codes[z, t] = codes[:, t * P : (t + 1) * P]
                 w1_planes[z, t] = plane[:, t * P : (t + 1) * P]
+            if z == 0:
+                gather_words(0)
+
+        w2_codes = shared.tile([P, 2 * N], U8, name="w2_codes", align_bytes=BURST, offset=W2_CODES_AT)
+        nc.sync.dma_start(w2_codes[:].bitcast(I32), w2_words[0].bitcast(I32))
+        w2_plane = shared.tile([P, N], U8, name="w2_plane", align_bytes=BURST, offset=W2_PLANE_AT)
+        nc.vector.memset(w2_plane[:].bitcast(I32), 0)
+        for q in range(QUADRANTS):
+            nc.sync.dma_start(w2_plane[32 * q : 32 * q + 4, :].bitcast(I32), w2_scales[0, 4 * q : 4 * q + 4, :].bitcast(I32))
 
         banks = [(0, range(0, 1)), (0, range(1, 2)), (0, range(2, 4))] + [(c, range(PACK)) for c in range(1, CHUNKS)]
         hidden = [psum.tile([P, len(tiles), CHUNK], F32, name=f"hidden{b}", tag=f"hidden{b}") for b, (c, tiles) in enumerate(banks)]

from contextlib import ExitStack

import concourse.mybir as mybir

K, T, S, H, N = 1024, 2048, 512, 512, 128
FLOPS = 2 * K * H * S + 2 * H * N * S

F32 = mybir.dt.float32
BF16 = mybir.dt.bfloat16
I32 = mybir.dt.int32
U32 = mybir.dt.uint32
U16 = mybir.dt.uint16
U8 = mybir.dt.uint8
FP8X4 = mybir.dt.float8_e4m3fn_x4
FP4X4 = mybir.dt.float4_e2m1fn_x4
GELU = mybir.ActivationFunctionType.Gelu_apprx_tanh

P = 128
PACK = 4
PASSES = K // (P * PACK)
QUADRANTS = 4
ROWS = 4
HALF = 256
CHUNK = 128
CHUNKS = S // CHUNK
TAIL = 64
RING = 2 * CHUNK

EARLY_ROWS = 2

BURST = 256
LAST_WEIGHTS_AT = 0
LAST_TABLE_AT = LAST_WEIGHTS_AT + 4 * (PACK - EARLY_ROWS) * H
PICKED_SCALES_AT = LAST_TABLE_AT - BURST
FIRST_WEIGHTS_AT = LAST_TABLE_AT + 4 * T
W2_CODES_AT = FIRST_WEIGHTS_AT
W2_PLANE_AT = W2_CODES_AT + 2 * N


def tile_picked_phmlp_gelu_p_kernel(tc, x_words, x_scales, w1, w2_words, w2_scales, offs, out):
    nc = tc.nc
    with ExitStack() as ctx:
        keep = ctx.enter_context(tc.tile_pool(name="keep", bufs=1))
        shared = ctx.enter_context(tc.tile_pool(name="shared", bufs=1))
        psum = ctx.enter_context(tc.psum_pool(name="psum", bufs=1))

        w1_rows = [w1[512 * z : 512 * (z + 1), :].rearrange("(p j) c -> p j c", j=PACK) for z in range(PASSES)]
        x_rows = [x_words[z].rearrange("p n t -> p (n t)").bitcast(I32) for z in range(PASSES)]

        scale_table = keep.tile([P, T], U8, name="scale_table", align_bytes=BURST)
        nc.vector.memset(scale_table[:].bitcast(I32), 0)

        w1_early = keep.tile([P, EARLY_ROWS, H], F32, name="w1_early", align_bytes=BURST)
        nc.sync.dma_start(w1_early[:], w1_rows[1][:, :EARLY_ROWS])
        lists = keep.tile([P, S // 16], U16, name="lists", align_bytes=BURST)
        nc.sync.dma_start(lists[:], offs)
        nc.sync.dma_start(scale_table[0:P:4, :].bitcast(I32), x_scales.bitcast(I32).rearrange("z q c -> q z c"))
        w1_first = shared.tile([P, PACK, H], F32, name="w1_first", align_bytes=BURST, offset=FIRST_WEIGHTS_AT)
        nc.sync.dma_start(w1_first[:], w1_rows[0])
        x_table = [keep.tile([P, T], I32, name="x_table0", align_bytes=BURST)]
        nc.sync.dma_start(x_table[0][:], x_rows[0])

        x_planes = [keep.tile([P, S], U8, name=f"x_plane{z}", align_bytes=BURST) for z in range(PASSES)]
        picked_scales = shared.tile([P, S], U8, name="picked_scales", align_bytes=BURST, offset=PICKED_SCALES_AT)
        nc.vector.tensor_copy(picked_scales[:], scale_table[:].indirect(lists[:]))
        for z in range(PASSES):
            nc.vector.tensor_copy(x_planes[z][:].bitcast(I32), picked_scales[:].bitcast(I32))

        def move_scales(z):
            for i in range(1, ROWS):
                nc.sync.dma_start(
                    x_planes[z][4 * z + i : P : 32, :].bitcast(I32),
                    x_planes[z][8 * i + 4 * z : P : 32, :].bitcast(I32),
                )

        move_scales(0)
        w1_late = shared.tile([P, PACK - EARLY_ROWS, H], F32, name="w1_late", align_bytes=BURST, offset=LAST_WEIGHTS_AT)
        nc.sync.dma_start(w1_late[:], w1_rows[1][:, EARLY_ROWS:])
        x_table.append(shared.tile([P, T], I32, name="x_table1", align_bytes=BURST, offset=LAST_TABLE_AT))
        nc.sync.dma_start(x_table[1][:], x_rows[1])
        move_scales(1)

        picked = [keep.tile([P, S], U32, name=f"picked{z}", align_bytes=64) for z in range(PASSES)]

        def gather_words(z):
            for half in range(S // HALF):
                entries = slice(half * HALF // 16, (half + 1) * HALF // 16)
                nc.vector.tensor_copy(picked[z][:, half * HALF : (half + 1) * HALF], x_table[z][:].bitcast(U32).indirect(lists[:, entries]))

        both = [nc.scalar.copy, nc.vector.tensor_copy]
        parts = [
            [(w1_first, slice(0, PACK), both)],
            [(w1_early, slice(0, EARLY_ROWS), [nc.scalar.copy] * 2), (w1_late, slice(EARLY_ROWS, PACK), both)],
        ]
        w1_codes, w1_planes = {}, {}
        for z in range(PASSES):
            grouped = keep.tile([P, PACK, P, PACK], BF16, name=f"w1_grouped{z}", align_bytes=64)
            codes = keep.tile([P, PACK * P], U32, name=f"w1_codes{z}", align_bytes=64)
            plane = keep.tile([P, PACK * P], U8, name=f"w1_plane{z}", align_bytes=64)
            for raw, rows, casts in parts[z]:
                src = raw[:].rearrange("p j (m t) -> p m j t", t=PACK)
                for pair, cast in enumerate(casts):
                    cast(grouped[:, 2 * pair : 2 * pair + 2, :, rows].rearrange("p t m j -> p m j t"), src[:, :, :, 2 * pair : 2 * pair + 2])
            for tiles in [range(PACK)] if z == 0 else [range(2, 4), range(0, 2)]:
                cols = slice(tiles.start * P, tiles.stop * P)
                nc.vector.quantize_mx(
                    out=codes[:, cols].bitcast(FP8X4),
                    scales=plane[:, cols],
                    in_=grouped[:, tiles.start : tiles.stop].rearrange("p t m j -> p (t m j)"),
                )
            for t in range(PACK):
                w1_codes[z, t] = codes[:, t * P : (t + 1) * P]
                w1_planes[z, t] = plane[:, t * P : (t + 1) * P]
            if z == 0:
                gather_words(0)

        w2_codes = shared.tile([P, 2 * N], U8, name="w2_codes", align_bytes=BURST, offset=W2_CODES_AT)
        nc.sync.dma_start(w2_codes[:].bitcast(I32), w2_words[0].bitcast(I32))
        w2_plane = shared.tile([P, N], U8, name="w2_plane", align_bytes=BURST, offset=W2_PLANE_AT)
        nc.vector.memset(w2_plane[:].bitcast(I32), 0)
        for q in range(QUADRANTS):
            nc.sync.dma_start(w2_plane[32 * q : 32 * q + 4, :].bitcast(I32), w2_scales[0, 4 * q : 4 * q + 4, :].bitcast(I32))

        banks = [(0, range(0, 1)), (0, range(1, 2)), (0, range(2, 4))] + [(c, range(PACK)) for c in range(1, CHUNKS)]
        hidden = [psum.tile([P, len(tiles), CHUNK], F32, name=f"hidden{b}", tag=f"hidden{b}") for b, (c, tiles) in enumerate(banks)]
        gather_words(1)
        for z in range(PASSES):
            for b, (c, tiles) in enumerate(banks):
                for t in tiles:
                    nc.tensor.matmul_mx(
                        out=hidden[b][:, t - tiles[0], :],
                        lhsT=w1_codes[z, t].bitcast(FP8X4),
                        lhsT_scale=w1_planes[z, t],
                        rhs=picked[z][:, c * CHUNK : (c + 1) * CHUNK].bitcast(FP8X4),
                        rhs_scale=x_planes[z][4 * z :, c * CHUNK : (c + 1) * CHUNK],
                        start=(z == 0 and t == tiles[0]),
                        stop=(z == PASSES - 1 and t == tiles[-1]),
                    )

        def gelu(dst, bank):
            nc.scalar.activation(
                dst.rearrange("p (n e) t -> p n t e", e=2),
                bank.rearrange("p t (n e) -> p n t e", e=2),
                GELU,
            )

        pieces = [(c * CHUNK, (c + 1) * CHUNK) for c in range(CHUNKS - 1)] + [(S - CHUNK, S - TAIL), (S - TAIL, S)]
        h_tiles = keep.tile([P, PACK, CHUNK], BF16, name="h_tiles", align_bytes=64)
        h_codes = keep.tile([P, RING], U32, name="h_codes", align_bytes=64)
        h_plane = keep.tile([P, RING], U8, name="h_plane", align_bytes=64)
        spare_banks = ["spare0", "spare1", "hidden0", "hidden1", "hidden2"]
        stores = [[1], [0], [2], [3, 4]]
        h_grouped, acc = {}, {}

        def activate(n):
            lo, hi = pieces[n]
            c = lo // CHUNK
            h_grouped[n] = keep.tile([P, hi - lo, PACK], BF16, name=f"h_grouped{n}", tag=f"h_grouped{n}", align_bytes=64)
            if c == 0:
                for b in range(3):
                    tiles = banks[b][1]
                    nc.scalar.activation(h_tiles[:, tiles.start : tiles.stop], hidden[b][:], GELU)
                nc.vector.tensor_copy(
                    h_grouped[n][:].rearrange("p (n e) t -> p n t e", e=PACK), h_tiles[:].rearrange("p t (n e) -> p n t e", e=PACK)
                )
            else:
                gelu(h_grouped[n][:], hidden[c + 2][:, :, lo - c * CHUNK : hi - c * CHUNK])

        def product(n):
            lo, hi = pieces[n]
            if n == 0:
                codes = keep.tile([P, CHUNK], U32, name="h_codes0", tag="h_grouped1", align_bytes=64)
                plane = keep.tile([P, CHUNK], U8, name="h_plane0", align_bytes=64)
                end = CHUNK
            else:
                codes, plane = h_codes, h_plane
                end = (hi - 1) % RING + 1
            made, read = slice(end - (hi - lo), end), slice(end - CHUNK, end)
            nc.vector.quantize_mx(out=codes[:, made].bitcast(FP8X4), scales=plane[:, made], in_=h_grouped[n][:].rearrange("p n t -> p (n t)"))
            acc[n] = psum.tile([N, CHUNK], F32, name=f"acc{n}", tag=spare_banks[n])
            nc.tensor.matmul_mx(
                out=acc[n][:],
                lhsT=w2_codes[:].bitcast(FP4X4),
                lhsT_scale=w2_plane[:],
                rhs=codes[:, read].bitcast(FP8X4),
                rhs_scale=plane[:, read],
                start=True,
                stop=True,
            )

        def store(group):
            first, last = pieces[group[0]][0], pieces[group[-1]][1]
            result = keep.tile([N, last - first], F32, name=f"result{group[0]}", align_bytes=BURST)
            for n in group:
                copy = nc.vector.tensor_copy if n in (1, 3, 4) else nc.scalar.copy
                lo, hi = pieces[n]
                copy(result[:, lo - first : hi - first], acc[n][:, CHUNK - (hi - lo) :])
            nc.sync.dma_start(out[:, first:last], result[:])

        for n in range(len(pieces)):
            activate(n)
        product(1)
        product(0)
        product(2)
        store(stores[0])
        product(3)
        product(4)
        store(stores[1])
        store(stores[2])
        store(stores[3])
